import numpy as np
import ml_dtypes


def mxq(x, axis, fmt="e4m3"):
    dtype, down = {"e4m3": (ml_dtypes.float8_e4m3fn, 7), "e5m2": (ml_dtypes.float8_e5m2, 14)}[fmt]
    v = np.moveaxis(np.asarray(x, np.float32).astype(ml_dtypes.bfloat16).astype(np.float64), axis, -1)
    blocks = v.reshape(v.shape[:-1] + (-1, 32))
    amax = np.abs(blocks).max(-1, keepdims=True)
    byte = np.maximum(np.where(amax > 0, np.frexp(amax)[1] - 1 + 127, 0) - down, 1)
    scale = np.exp2(byte - 127.0)
    codes = (blocks / scale).astype(np.float32).astype(dtype).astype(np.float64)
    return np.moveaxis((codes * scale).reshape(v.shape), -1, axis)


WIDE = False


def mx_kscale(k):
    if not WIDE:
        return np.ones(k)
    levels = np.array([10, -10, 5, -5, 0])
    if k % 512:
        return np.exp2(np.random.permutation(np.resize(levels, k // 32))).repeat(32)
    a = np.empty((k // 512, 16))
    for p in range(k // 512):
        a[p, :8] = np.random.permutation(np.resize(levels, 8))
        for g in range(8):
            far = levels[np.abs(levels - a[p, g]) >= 10]
            a[p, g + 8] = far[np.random.randint(len(far))]
    return np.exp2(a.ravel()).repeat(32)


def f64(x):
    return np.asarray(x).astype(np.float64)


def striped(idx):
    return np.tile(idx.reshape(-1, 16).T, (8, 1)).astype(np.uint16)


def unstriped(offs):
    return offs[:16].T.reshape(-1).astype(np.int64)


def striped8(idx):
    return np.concatenate([x.reshape(-1, 16).T for x in idx]).astype(np.uint16)


def runs(offs, k):
    lists = np.stack([offs[16 * r : 16 * r + 16].T.reshape(-1) for r in range(8)]).astype(np.int64)
    return lists[np.arange(k) % 512 // 64]


def pack_weight(w):
    k, n = w.shape
    w = f64(np.asarray(w, np.float32).astype(ml_dtypes.bfloat16)).reshape(k // 32, 32, n)
    amax = np.abs(w).max(1)
    byte = np.clip(np.where(amax > 0, np.frexp(amax)[1] - 1 + 127 - 7, 1), 1, 254)
    scaled = (w * np.exp2(127.0 - byte)[:, None, :]).reshape(k, n).astype(np.float32)
    words = np.ascontiguousarray(scaled.reshape(k // 512, 128, 4, n).transpose(0, 1, 3, 2)).astype(ml_dtypes.float8_e4m3fn).view(np.uint8)
    return words, np.ascontiguousarray(byte.astype(np.uint8).reshape(k // 512, 16, n))


def unpack_weight(words, scales):
    g, p, n, _ = words.shape
    vals = np.ascontiguousarray(words).view(ml_dtypes.float8_e4m3fn).astype(np.float64) * np.repeat(np.exp2(scales.astype(np.float64) - 127.0), 8, axis=1)[..., None]
    return vals.transpose(0, 1, 3, 2).reshape(g * 512, n)


def relu(v):
    return np.maximum(v, 0.0)


K, T, S, N, H = 512, 2048, 512, 512, 512


def setup_inputs():
    n = np.random.standard_normal
    s = mx_kscale(K)[:, None]
    u = mx_kscale(H)
    packed_xT = pack_weight(n((K, T)) * s)
    return {
        "x_words": packed_xT[0],
        "x_scales": packed_xT[1],
        "w1": (n((K, H)) / np.sqrt(K) / s * u).astype(np.float32),
        "w2": (n((K, N)) / np.sqrt(K) / s).astype(np.float32),
        "w3": (n((H, N)) / np.sqrt(H) / u[:, None]).astype(np.float32),
        "offs": striped(np.random.permutation(T)[:S]),
        "in1": striped8(np.stack([np.random.permutation(S) for _ in range(8)])),
        "in2": striped8(np.stack([np.random.permutation(S) for _ in range(8)])),
        "rev": striped8(np.stack([np.random.permutation(S) for _ in range(8)])),
    }


def reference(x_words, x_scales, w1, w2, w3, offs, in1, in2, rev):
    xq = unpack_weight(x_words, x_scales)[:, unstriped(offs)]
    h0 = mxq(f64(w2), 0, "e4m3").T @ xq
    y = mxq(f64(w1), 0, "e4m3").T @ xq
    z = y[np.arange(H)[:, None], runs(in1, H)] + y[np.arange(H)[:, None], runs(in2, H)] - (y[np.arange(H)[:, None], runs(rev, H)])
    o = h0 + (mxq(f64(w3), 0, "e4m3").T @ mxq(z, 0, "e4m3"))
    return relu(o)

@@ -1,0 +1,161 @@
+from contextlib import ExitStack
+
+import concourse.mybir as mybir
+
+F32 = mybir.dt.float32
+BF16 = mybir.dt.bfloat16
+I32 = mybir.dt.int32
+U32 = mybir.dt.uint32
+U16 = mybir.dt.uint16
+U8 = mybir.dt.uint8
+FP8X4 = mybir.dt.float8_e4m3fn_x4
+ADD = mybir.AluOpType.add
+SUB = mybir.AluOpType.subtract
+RELU = mybir.ActivationFunctionType.Relu
+
+P = 128
+PACK = 4
+K, T, S, N, H = 512, 2048, 512, 512, 512
+PER_COL = 16
+SLICES = ((0, 256), (256, 128), (384, 128))
+FLOPS = 2 * S * (K * N + K * H + H * N)
+
+
+def tile_picked_dmpnn8_relu_p_kernel(
+    tc, x_words, x_scales, w1, w2, w3, offs, in1, in2, rev, out
+):
+    nc = tc.nc
+    with ExitStack() as ctx:
+        keep = ctx.enter_context(tc.tile_pool(name="keep", bufs=1))
+        psum = ctx.enter_context(tc.psum_pool(name="psum", bufs=1))
+
+        offs_sb = keep.tile([P, S // PER_COL], U16, name="offs_sb")
+        in1_sb = keep.tile([P, S // PER_COL], U16, name="in1_sb")
+        in2_sb = keep.tile([P, S // PER_COL], U16, name="in2_sb")
+        rev_sb = keep.tile([P, S // PER_COL], U16, name="rev_sb")
+        words_all = keep.tile([P, T], I32, name="words_all")
+        scales_all = keep.tile([P, T], U8, name="scales_all")
+        w1_raw = [keep.tile([P, PACK, H // 2], F32, name="w1_raw%d" % h) for h in range(2)]
+        w2_raw = keep.tile([P, PACK, N], F32, name="w2_raw")
+        w3_raw = keep.tile([P, PACK, N], F32, name="w3_raw")
+
+        nc.vector.memset(scales_all[:].bitcast(I32), 0)
+        nc.sync.dma_start(offs_sb[:], offs)
+        for q in range(4):
+            nc.sync.dma_start(
+                out=scales_all[32 * q : 32 * q + 4, :].bitcast(I32),
+                in_=x_scales[0, 4 * q : 4 * q + 4, :].bitcast(I32),
+            )
+        w1_rows = w1.rearrange("(p j) c -> p j c", j=PACK)
+        for h in range(2):
+            nc.sync.dma_start(out=w1_raw[h][:], in_=w1_rows[:, :, h * (H // 2) : (h + 1) * (H // 2)])
+        nc.sync.dma_start(out=words_all[:], in_=x_words[0].rearrange("p n t -> p (n t)").bitcast(I32))
+        nc.sync.dma_start(rev_sb[:], rev)
+        nc.sync.dma_start(in1_sb[:], in1)
+        nc.sync.dma_start(in2_sb[:], in2)
+        nc.sync.dma_start(out=w2_raw[:], in_=w2.rearrange("(p j) c -> p j c", j=PACK))
+        nc.sync.dma_start(out=w3_raw[:], in_=w3.rearrange("(p j) c -> p j c", j=PACK))
+
+        def quantize(name, grouped, width, tag=None):
+            codes = keep.tile([P, width], U32, name=name + "_codes", tag=tag or name + "_codes", align_bytes=64)
+            scales = keep.tile([P, width], U8, name=name + "_scales", align_bytes=64)
+            nc.vector.quantize_mx(out=codes[:].bitcast(FP8X4), scales=scales[:], in_=grouped)
+            return codes, scales
+
+        x_sc = keep.tile([P, S], U8, name="x_sc", align_bytes=64)
+        nc.vector.tensor_copy(x_sc[:], scales_all[:].indirect(offs_sb[:]))
+
+        w1_grp = keep.tile([P, PACK, P, PACK], BF16, name="w1_grp", align_bytes=64)
+        for h, copy in enumerate((nc.scalar.copy, nc.vector.tensor_copy)):
+            copy(
+                w1_grp[:, :, h * 64 : (h + 1) * 64, :].rearrange("p t m j -> p m j t"),
+                w1_raw[h][:].rearrange("p j (m t) -> p m j t", t=PACK),
+            )
+        w1_q, w1_s = quantize("w1", w1_grp[:].rearrange("p t m j -> p (t m j)"), H)
+
+        x_q = keep.tile([P, S], U32, name="x_q", align_bytes=64)
+        for h in range(2):
+            nc.vector.tensor_copy(
+                x_q[:, h * 256 : (h + 1) * 256],
+                words_all[:].bitcast(U32).indirect(offs_sb[:, h * 16 : (h + 1) * 16]),
+            )
+
+        def mx(dst, lq, ls, m, rq, rs, cols, start, stop):
+            nc.tensor.matmul_mx(
+                out=dst,
+                lhsT=lq[:, m * P : (m + 1) * P].bitcast(FP8X4),
+                lhsT_scale=ls[:, m * P : (m + 1) * P],
+                rhs=rq[:, cols].bitcast(FP8X4),
+                rhs_scale=rs[:, cols],
+                start=start,
+                stop=stop,
+            )
+
+        y = [keep.tile([P, S], F32, name="y%d" % t) for t in range(PACK)]
+        for h in range(2):
+            cols = slice(h * 256, (h + 1) * 256)
+            bank = psum.tile([P, 512], F32, name="y0_bank%d" % h, tag="bank%d" % (4 * h))
+            mx(bank[:, 0:256], w1_q, w1_s, 0, x_q, x_sc, cols, True, True)
+            nc.scalar.copy(y[0][:, cols], bank[:, 0:256])
+        for t in range(1, PACK):
+            bank = psum.tile([P, 512], F32, name="y_bank%d" % t, tag="bank%d" % t)
+            mx(bank[:], w1_q, w1_s, t, x_q, x_sc, slice(0, S), True, True)
+            nc.scalar.copy(y[t][:], bank[:])
+
+        def cast_weight(name, raw):
+            grp = keep.tile([P, N, PACK], BF16, name=name + "_grp", align_bytes=64)
+            nc.scalar.copy(
+                grp[:].rearrange("p (c i) j -> p c j i", i=4),
+                raw[:].rearrange("p j (c i) -> p c j i", i=4),
+            )
+            return quantize(name, grp[:].rearrange("p c j -> p (c j)"), N)
+
+        w2_q, w2_s = cast_weight("w2", w2_raw)
+        w3_q, w3_s = cast_weight("w3", w3_raw)
+
+        out_rows = out.rearrange("(u p) j -> p u j", p=P)
+        for s, (c0, n) in enumerate(SLICES):
+            last = s == len(SLICES) - 1
+            cols = slice(c0, c0 + n)
+            lcols = slice(c0 // PER_COL, (c0 + n) // PER_COL)
+            gb = keep.tile([P, PACK, n], F32, name="gb%d" % s)
+            z = keep.tile([P, PACK, n], F32, name="z%d" % s, tag="z%d" % (s % 2))
+            for pair in range(2):
+                ts = (2 * pair, 2 * pair + 1)
+                ga = keep.tile([P, 2, n], F32, name="ga%d_%d" % (s, pair), tag=("z%d" % ((s + 1) % 2) if pair else "ga"))
+                for t in ts:
+                    nc.vector.tensor_copy(ga[:, t % 2, :], y[t][:].indirect(rev_sb[:, lcols]))
+                for t in ts:
+                    nc.vector.tensor_tensor(gb[:, t, :], y[t][:].indirect(in1_sb[:, lcols]), ga[:, t % 2, :], SUB)
+                for t in ts:
+                    nc.vector.tensor_tensor(z[:, t, :], y[t][:].indirect(in2_sb[:, lcols]), gb[:, t, :], ADD)
+            z_grp = keep.tile([P, n, PACK], BF16, name="z_grp%d" % s, tag="zq%d" % s, align_bytes=64)
+            copy = nc.vector.tensor_copy if last else nc.scalar.copy
+            copy(
+                z_grp[:].rearrange("p (c i) t -> p c t i", i=4),
+                z[:].rearrange("p t (c i) -> p c t i", i=4),
+            )
+            z_q, z_s = quantize("z%d" % s, z_grp[:].rearrange("p c t -> p (c t)"), n, "zq%d" % (s + 1))
+            res = keep.tile([P, PACK, n], F32, name="res%d" % s)
+            if last:
+                banks = [psum.tile([P, 512], F32, name="o_bank%d" % u, tag="bank%d" % u) for u in range(4)]
+                for u in range(4):
+                    mx(banks[u][:, 0:n], w2_q, w2_s, u, x_q, x_sc, cols, True, False)
+                for u in range(4):
+                    mx(banks[u][:, 0:n], w3_q, w3_s, u, z_q, z_s, slice(0, n), False, True)
+                    if u % 2 == 0:
+                        nc.scalar.activation(res[:, u, :], banks[u][:, 0:n], RELU)
+                    else:
+                        nc.vector.tensor_scalar_max(res[:, u, :], banks[u][:, 0:n], 0.0)
+                nc.sync.dma_start(out=out_rows[:, :, cols], in_=res[:])
+            else:
+                per_bank = 512 // n
+                for b in range(4 // per_bank):
+                    bank = psum.tile([P, per_bank, n], F32, name="o_bank%d_%d" % (s, b), tag="bank%d" % (5 + 2 * s + b))
+                    for v in range(per_bank):
+                        u = b * per_bank + v
+                        mx(bank[:, v, :], w2_q, w2_s, u, x_q, x_sc, cols, True, False)
+                        mx(bank[:, v, :], w3_q, w3_s, u, z_q, z_s, slice(0, n), False, True)
+                    us = slice(b * per_bank, (b + 1) * per_bank)
+                    nc.scalar.activation(res[:, us, :], bank[:], RELU)
+                nc.sync.dma_start(out=out_rows[:, :, cols], in_=res[:])

@@ -18,6 +18,7 @@ PACK = 4
 K, T, S, N, H = 512, 2048, 512, 512, 512
 PER_COL = 16
 SLICES = ((0, 256), (256, 128), (384, 128))
+GB_TAGS = ("gb", "w2_raw", "w3_raw", "z0", "gb", "z1")
 FLOPS = 2 * S * (K * N + K * H + H * N)
 
 
@@ -118,24 +119,24 @@ def tile_picked_dmpnn8_relu_p_kernel(
             last = s == len(SLICES) - 1
             cols = slice(c0, c0 + n)
             lcols = slice(c0 // PER_COL, (c0 + n) // PER_COL)
-            gb = keep.tile([P, PACK, n], F32, name="gb%d" % s)
-            z = keep.tile([P, PACK, n], F32, name="z%d" % s, tag="z%d" % (s % 2))
+            z = keep.tile([P, PACK, n], F32, name="z%d" % s)
             for pair in range(2):
                 ts = (2 * pair, 2 * pair + 1)
-                ga = keep.tile([P, 2, n], F32, name="ga%d_%d" % (s, pair), tag=("z%d" % ((s + 1) % 2) if pair else "ga"))
+                ga = keep.tile([P, 2, n], F32, name="ga%d_%d" % (s, pair), tag="ga")
+                gb = keep.tile([P, 2, n], F32, name="gb%d_%d" % (s, pair), tag=GB_TAGS[2 * s + pair])
                 for t in ts:
                     nc.vector.tensor_copy(ga[:, t % 2, :], y[t][:].indirect(rev_sb[:, lcols]))
                 for t in ts:
-                    nc.vector.tensor_tensor(gb[:, t, :], y[t][:].indirect(in1_sb[:, lcols]), ga[:, t % 2, :], SUB)
+                    nc.vector.tensor_tensor(gb[:, t % 2, :], y[t][:].indirect(in1_sb[:, lcols]), ga[:, t % 2, :], SUB)
                 for t in ts:
-                    nc.vector.tensor_tensor(z[:, t, :], y[t][:].indirect(in2_sb[:, lcols]), gb[:, t, :], ADD)
+                    nc.vector.tensor_tensor(z[:, t, :], y[t][:].indirect(in2_sb[:, lcols]), gb[:, t % 2, :], ADD)
             z_grp = keep.tile([P, n, PACK], BF16, name="z_grp%d" % s, tag="zq%d" % s, align_bytes=64)
             copy = nc.vector.tensor_copy if last else nc.scalar.copy
             copy(
                 z_grp[:].rearrange("p (c i) t -> p c t i", i=4),
                 z[:].rearrange("p t (c i) -> p c t i", i=4),
             )
-            z_q, z_s = quantize("z%d" % s, z_grp[:].rearrange("p c t -> p (c t)"), n, "zq%d" % (s + 1))
+            z_q, z_s = quantize("z%d" % s, z_grp[:].rearrange("p c t -> p (c t)"), n, "zq%d" % (s + 1) if s == 0 else None)
             res = keep.tile([P, PACK, n], F32, name="res%d" % s)
             if last:
                 banks = [psum.tile([P, 512], F32, name="o_bank%d" % u, tag="bank%d" % u) for u in range(4)]
@@ -147,7 +148,7 @@ def tile_picked_dmpnn8_relu_p_kernel(
                         nc.scalar.activation(res[:, u, :], banks[u][:, 0:n], RELU)
                     else:
                         nc.vector.tensor_scalar_max(res[:, u, :], banks[u][:, 0:n], 0.0)
-                nc.sync.dma_start(out=out_rows[:, :, cols], in_=res[:])
+                        nc.sync.dma_start(out=out_rows[:, u - 1 : u + 1, cols], in_=res[:, u - 1 : u + 1, :])
             else:
                 per_bank = 512 // n
                 for b in range(4 // per_bank):

@@ -17,8 +17,8 @@ P = 128
 PACK = 4
 K, T, S, N, H = 512, 2048, 512, 512, 512
 PER_COL = 16
-SLICES = ((0, 256), (256, 128), (384, 128))
-GB_TAGS = ("gb", "w2_raw", "w3_raw", "z0", "gb", "z1")
+HALF = S // 2
+QUARTER = S // 4
 FLOPS = 2 * S * (K * N + K * H + H * N)
 
 
@@ -30,133 +30,185 @@ def tile_picked_dmpnn8_relu_p_kernel(
         keep = ctx.enter_context(tc.tile_pool(name="keep", bufs=1))
         psum = ctx.enter_context(tc.psum_pool(name="psum", bufs=1))
 
-        offs_sb = keep.tile([P, S // PER_COL], U16, name="offs_sb")
-        in1_sb = keep.tile([P, S // PER_COL], U16, name="in1_sb")
-        in2_sb = keep.tile([P, S // PER_COL], U16, name="in2_sb")
-        rev_sb = keep.tile([P, S // PER_COL], U16, name="rev_sb")
-        words_all = keep.tile([P, T], I32, name="words_all")
-        scales_all = keep.tile([P, T], U8, name="scales_all")
-        w1_raw = [keep.tile([P, PACK, H // 2], F32, name="w1_raw%d" % h) for h in range(2)]
-        w2_raw = keep.tile([P, PACK, N], F32, name="w2_raw")
-        w3_raw = keep.tile([P, PACK, N], F32, name="w3_raw")
+        def sbuf(name, shape, dtype, tag=None):
+            return keep.tile([P] + shape, dtype, name=name, tag=tag or name, align_bytes=64)
+
+        offs_sb = sbuf("offs_sb", [S // PER_COL], U16)
+        in1_sb = sbuf("in1_sb", [S // PER_COL], U16)
+        in2_sb = sbuf("in2_sb", [S // PER_COL], U16)
+        rev_sb = sbuf("rev_sb", [S // PER_COL], U16)
+        words_all = sbuf("words_all", [T], I32)
+        scales_all = sbuf("scales_all", [T], U8)
+        w1_raw = [sbuf("w1_raw%d" % h, [2, H], F32) for h in range(2)]
+        w2_raw = sbuf("w2_raw", [PACK, N], F32)
+        w3_raw = sbuf("w3_raw", [PACK, N], F32)
+        y_wide = [sbuf("y_wide%d" % t, [2 * S], F32) for t in range(PACK)]
 
         nc.vector.memset(scales_all[:].bitcast(I32), 0)
+        words_hbm = x_words[0].rearrange("p n t -> p (n t)").bitcast(I32)
+        nc.sync.dma_start(out=words_all[:, 0 : T // 2], in_=words_hbm[:, 0 : T // 2])
         nc.sync.dma_start(offs_sb[:], offs)
-        for q in range(4):
-            nc.sync.dma_start(
-                out=scales_all[32 * q : 32 * q + 4, :].bitcast(I32),
-                in_=x_scales[0, 4 * q : 4 * q + 4, :].bitcast(I32),
-            )
+        for r in range(4):
+            nc.sync.dma_start(out=scales_all[r:P:32, :].bitcast(I32), in_=x_scales[0, r:16:4, :].bitcast(I32))
+        nc.sync.dma_start(out=words_all[:, T // 2 : T], in_=words_hbm[:, T // 2 : T])
         w1_rows = w1.rearrange("(p j) c -> p j c", j=PACK)
         for h in range(2):
-            nc.sync.dma_start(out=w1_raw[h][:], in_=w1_rows[:, :, h * (H // 2) : (h + 1) * (H // 2)])
-        nc.sync.dma_start(out=words_all[:], in_=x_words[0].rearrange("p n t -> p (n t)").bitcast(I32))
+            nc.sync.dma_start(out=w1_raw[h][:], in_=w1_rows[:, 2 * h : 2 * h + 2, :])
         nc.sync.dma_start(rev_sb[:], rev)
         nc.sync.dma_start(in1_sb[:], in1)
         nc.sync.dma_start(in2_sb[:], in2)
-        nc.sync.dma_start(out=w2_raw[:], in_=w2.rearrange("(p j) c -> p j c", j=PACK))
-        nc.sync.dma_start(out=w3_raw[:], in_=w3.rearrange("(p j) c -> p j c", j=PACK))
+        for raw, w in ((w2_raw, w2), (w3_raw, w3)):
+            for j in (0, 2):
+                nc.sync.dma_start(out=raw[:, j : j + 2, :], in_=w.rearrange("(p j) c -> p j c", j=PACK)[:, j : j + 2, :])
+        for t in range(PACK):
+            nc.vector.memset(y_wide[t][:, S : 2 * S], 0.0)
+
+        x_sc = sbuf("x_sc", [S], U8)
+        x_q = sbuf("x_q", [S], U32)
+        nc.vector.tensor_copy(x_sc[:], scales_all[:].indirect(offs_sb[:]))
+        nc.vector.tensor_copy(x_q[:], words_all[:].bitcast(U32).indirect(offs_sb[:]))
 
         def quantize(name, grouped, width, tag=None):
-            codes = keep.tile([P, width], U32, name=name + "_codes", tag=tag or name + "_codes", align_bytes=64)
-            scales = keep.tile([P, width], U8, name=name + "_scales", align_bytes=64)
+            codes = sbuf(name + "_codes", [width], U32, tag)
+            scales = sbuf(name + "_scales", [width], U8)
             nc.vector.quantize_mx(out=codes[:].bitcast(FP8X4), scales=scales[:], in_=grouped)
             return codes, scales
 
-        x_sc = keep.tile([P, S], U8, name="x_sc", align_bytes=64)
-        nc.vector.tensor_copy(x_sc[:], scales_all[:].indirect(offs_sb[:]))
-
-        w1_grp = keep.tile([P, PACK, P, PACK], BF16, name="w1_grp", align_bytes=64)
-        for h, copy in enumerate((nc.scalar.copy, nc.vector.tensor_copy)):
-            copy(
-                w1_grp[:, :, h * 64 : (h + 1) * 64, :].rearrange("p t m j -> p m j t"),
-                w1_raw[h][:].rearrange("p j (m t) -> p m j t", t=PACK),
-            )
-        w1_q, w1_s = quantize("w1", w1_grp[:].rearrange("p t m j -> p (t m j)"), H)
-
-        x_q = keep.tile([P, S], U32, name="x_q", align_bytes=64)
-        for h in range(2):
-            nc.vector.tensor_copy(
-                x_q[:, h * 256 : (h + 1) * 256],
-                words_all[:].bitcast(U32).indirect(offs_sb[:, h * 16 : (h + 1) * 16]),
-            )
-
-        def mx(dst, lq, ls, m, rq, rs, cols, start, stop):
+        def mx(dst, left, m, right, cols, start, stop):
             nc.tensor.matmul_mx(
                 out=dst,
-                lhsT=lq[:, m * P : (m + 1) * P].bitcast(FP8X4),
-                lhsT_scale=ls[:, m * P : (m + 1) * P],
-                rhs=rq[:, cols].bitcast(FP8X4),
-                rhs_scale=rs[:, cols],
+                lhsT=left[0][:, m * P : (m + 1) * P].bitcast(FP8X4),
+                lhsT_scale=left[1][:, m * P : (m + 1) * P],
+                rhs=right[0][:, cols].bitcast(FP8X4),
+                rhs_scale=right[1][:, cols],
                 start=start,
                 stop=stop,
             )
 
-        y = [keep.tile([P, S], F32, name="y%d" % t) for t in range(PACK)]
-        for h in range(2):
-            cols = slice(h * 256, (h + 1) * 256)
-            bank = psum.tile([P, 512], F32, name="y0_bank%d" % h, tag="bank%d" % (4 * h))
-            mx(bank[:, 0:256], w1_q, w1_s, 0, x_q, x_sc, cols, True, True)
-            nc.scalar.copy(y[0][:, cols], bank[:, 0:256])
-        for t in range(1, PACK):
-            bank = psum.tile([P, 512], F32, name="y_bank%d" % t, tag="bank%d" % t)
-            mx(bank[:], w1_q, w1_s, t, x_q, x_sc, slice(0, S), True, True)
-            nc.scalar.copy(y[t][:], bank[:])
+        plane_sets = ((0, 1), (1, 1), (2, 2))
+        w1_grp = [sbuf("w1_grp%d" % t0, [n, P, PACK], BF16) for t0, n in plane_sets]
 
-        def cast_weight(name, raw):
-            grp = keep.tile([P, N, PACK], BF16, name=name + "_grp", align_bytes=64)
-            nc.scalar.copy(
-                grp[:].rearrange("p (c i) j -> p c j i", i=4),
-                raw[:].rearrange("p j (c i) -> p c j i", i=4),
+        def cast_w1(copy, g, h):
+            t0, n = plane_sets[g]
+            copy(
+                w1_grp[g][:].rearrange("p t m j -> p m j t")[:, :, 2 * h : 2 * h + 2, :],
+                w1_raw[h][:].rearrange("p j (m t) -> p m j t", t=PACK)[:, :, :, t0 : t0 + n],
             )
+
+        for g in range(3):
+            cast_w1(nc.scalar.copy, g, 0)
+        cast_w1(nc.vector.tensor_copy, 0, 1)
+        cast_w1(nc.vector.tensor_copy, 1, 1)
+        cast_w1(nc.scalar.copy, 2, 1)
+        w1_mx = [
+            quantize("w1_%d" % g, w1_grp[g][:].rearrange("p t m j -> p (t m j)"), plane_sets[g][1] * P) for g in range(3)
+        ]
+        x_mx = (x_q, x_sc)
+
+        for i in range(4):
+            cols = slice(i * QUARTER, (i + 1) * QUARTER)
+            bank = psum.tile([P, QUARTER], F32, name="y0_bank%d" % i, tag="bank%d" % (4 + i))
+            mx(bank[:], w1_mx[0], 0, x_mx, cols, True, True)
+            (nc.vector.tensor_copy, nc.scalar.copy)[i % 2](y_wide[0][:, cols], bank[:])
+        for t, (g, m) in ((1, (1, 0)), (2, (2, 0)), (3, (2, 1))):
+            bank = psum.tile([P, S], F32, name="y_bank%d" % t, tag="bank%d" % t)
+            mx(bank[:], w1_mx[g], m, x_mx, slice(0, S), True, True)
+            nc.scalar.copy(y_wide[t][:, 0:S], bank[:])
+
+        def weave(copy, dst, src):
+            copy(dst.rearrange("p (c i) t -> p c t i", i=4), src.rearrange("p t (c i) -> p c t i", i=4))
+
+        def weight(name, raw):
+            grp = sbuf(name + "_grp", [N, PACK], BF16)
+            weave(nc.scalar.copy, grp[:], raw[:])
             return quantize(name, grp[:].rearrange("p c j -> p (c j)"), N)
 
-        w2_q, w2_s = cast_weight("w2", w2_raw)
-        w3_q, w3_s = cast_weight("w3", w3_raw)
+        w2_mx = weight("w2", w2_raw)
+        w3_mx = weight("w3", w3_raw)
+
+        y = [sbuf("y%d" % t, [S], F32) for t in range(PACK)]
+        for t in range(PACK):
+            nc.scalar.copy(y[t][:], y_wide[t][:, 0:S])
+
+        def add_in2(z, windows, part, c0, n):
+            for v in range(2):
+                offsets = in2_sb[:, c0 // PER_COL : (c0 + n) // PER_COL]
+                nc.vector.tensor_tensor(z[:, v, :], windows[v][:].indirect(offsets), part[:, v, c0 : c0 + n], ADD)
+
+        parts = []
+        z0_grp = sbuf("z0_grp", [HALF, PACK], BF16, "w3_raw")
+        for pair in range(2):
+            windows = y_wide[2 * pair : 2 * pair + 2]
+            back = sbuf("back%d" % pair, [2, S], F32, "back")
+            parts.append(sbuf("part%d" % pair, [2, S], F32))
+            for v in range(2):
+                nc.vector.tensor_copy(back[:, v, :], windows[v][:].indirect(rev_sb[:]))
+            for v in range(2):
+                nc.vector.tensor_tensor(parts[pair][:, v, :], windows[v][:].indirect(in1_sb[:]), back[:, v, :], SUB)
+            z0 = sbuf("z0_%d" % pair, [2, HALF], F32)
+            add_in2(z0, windows, parts[pair], 0, HALF)
+            weave(nc.scalar.copy, z0_grp[:, :, 2 * pair : 2 * pair + 2], z0[:])
+        z0_mx = quantize("z0", z0_grp[:].rearrange("p c t -> p (c t)"), HALF)
 
         out_rows = out.rearrange("(u p) j -> p u j", p=P)
-        for s, (c0, n) in enumerate(SLICES):
-            last = s == len(SLICES) - 1
-            cols = slice(c0, c0 + n)
-            lcols = slice(c0 // PER_COL, (c0 + n) // PER_COL)
-            z = keep.tile([P, PACK, n], F32, name="z%d" % s)
-            for pair in range(2):
-                ts = (2 * pair, 2 * pair + 1)
-                ga = keep.tile([P, 2, n], F32, name="ga%d_%d" % (s, pair), tag="ga")
-                gb = keep.tile([P, 2, n], F32, name="gb%d_%d" % (s, pair), tag=GB_TAGS[2 * s + pair])
-                for t in ts:
-                    nc.vector.tensor_copy(ga[:, t % 2, :], y[t][:].indirect(rev_sb[:, lcols]))
-                for t in ts:
-                    nc.vector.tensor_tensor(gb[:, t % 2, :], y[t][:].indirect(in1_sb[:, lcols]), ga[:, t % 2, :], SUB)
-                for t in ts:
-                    nc.vector.tensor_tensor(z[:, t, :], y[t][:].indirect(in2_sb[:, lcols]), gb[:, t % 2, :], ADD)
-            z_grp = keep.tile([P, n, PACK], BF16, name="z_grp%d" % s, tag="zq%d" % s, align_bytes=64)
-            copy = nc.vector.tensor_copy if last else nc.scalar.copy
-            copy(
-                z_grp[:].rearrange("p (c i) t -> p c t i", i=4),
-                z[:].rearrange("p t (c i) -> p c t i", i=4),
-            )
-            z_q, z_s = quantize("z%d" % s, z_grp[:].rearrange("p c t -> p (c t)"), n, "zq%d" % (s + 1) if s == 0 else None)
-            res = keep.tile([P, PACK, n], F32, name="res%d" % s)
-            if last:
-                banks = [psum.tile([P, 512], F32, name="o_bank%d" % u, tag="bank%d" % u) for u in range(4)]
-                for u in range(4):
-                    mx(banks[u][:, 0:n], w2_q, w2_s, u, x_q, x_sc, cols, True, False)
-                for u in range(4):
-                    mx(banks[u][:, 0:n], w3_q, w3_s, u, z_q, z_s, slice(0, n), False, True)
-                    if u % 2 == 0:
-                        nc.scalar.activation(res[:, u, :], banks[u][:, 0:n], RELU)
-                    else:
-                        nc.vector.tensor_scalar_max(res[:, u, :], banks[u][:, 0:n], 0.0)
-                        nc.sync.dma_start(out=out_rows[:, u - 1 : u + 1, cols], in_=res[:, u - 1 : u + 1, :])
-            else:
-                per_bank = 512 // n
-                for b in range(4 // per_bank):
-                    bank = psum.tile([P, per_bank, n], F32, name="o_bank%d_%d" % (s, b), tag="bank%d" % (5 + 2 * s + b))
-                    for v in range(per_bank):
-                        u = b * per_bank + v
-                        mx(bank[:, v, :], w2_q, w2_s, u, x_q, x_sc, cols, True, False)
-                        mx(bank[:, v, :], w3_q, w3_s, u, z_q, z_s, slice(0, n), False, True)
-                    us = slice(b * per_bank, (b + 1) * per_bank)
-                    nc.scalar.activation(res[:, us, :], bank[:], RELU)
-                nc.sync.dma_start(out=out_rows[:, :, cols], in_=res[:])
+
+        def open_banks(name, tags, c0, n):
+            per_bank = PACK // len(tags)
+            banks = [psum.tile([P, per_bank, n], F32, name="%s_%d" % (name, b), tag=tag) for b, tag in enumerate(tags)]
+            for u in range(PACK):
+                mx(banks[u // per_bank][:, u % per_bank, :], w2_mx, u, x_mx, slice(c0, c0 + n), u % per_bank == 0, False)
+            return banks
+
+        def close_banks(banks, z_mx, n):
+            per_bank = PACK // len(banks)
+            for u in range(PACK):
+                b, v = divmod(u, per_bank)
+                mx(banks[b][:, v, :], w3_mx, u, z_mx, slice(0, n), False, v == per_bank - 1)
+
+        def relu_scalar(dst, src):
+            nc.scalar.activation(dst, src, RELU)
+
+        def relu_vector(dst, src):
+            nc.vector.tensor_scalar_max(dst, src, 0.0)
+
+        def leave(name, relu, bank, u0, rows, c0, n, per_store, tag=None):
+            res = sbuf(name, [rows, n], F32, tag)
+            relu(res[:], bank[:])
+            for v in range(0, rows, per_store):
+                nc.sync.dma_start(
+                    out=out_rows[:, u0 + v : u0 + v + per_store, c0 : c0 + n], in_=res[:, v : v + per_store, :]
+                )
+
+        banks0 = [psum.tile([P, 2, HALF], F32, name="o0_%d" % b, tag="bank%d" % b) for b in range(2)]
+        first = slice(0, HALF)
+        for b, order in enumerate(((0, 0, 1, 1), (1, 0, 1, 0))):
+            for i, second in enumerate(order):
+                v = (i % 2, i // 2)[b]
+                left, right = ((w2_mx, x_mx), (w3_mx, z0_mx))[second]
+                mx(banks0[b][:, v, :], left, 2 * b + v, right, first, i == 0, i == 3)
+        banks1 = open_banks("o1", ("bank2", "bank3"), HALF, QUARTER)
+        banks2 = open_banks("o2", ("bank4", "bank5", "bank6", "bank7"), HALF + QUARTER, QUARTER)
+        leave("res0a", relu_scalar, banks0[0], 0, 2, 0, HALF, 1)
+
+        z1 = sbuf("z1", [PACK, QUARTER], F32, "z0_1")
+        for pair in range(2):
+            add_in2(z1[:, 2 * pair : 2 * pair + 2, :], y[2 * pair : 2 * pair + 2], parts[pair], HALF, QUARTER)
+        z2 = sbuf("z2", [PACK, QUARTER], F32, "w3_raw")
+        for pair in range(2):
+            add_in2(z2[:, 2 * pair : 2 * pair + 2, :], y[2 * pair : 2 * pair + 2], parts[pair], HALF + QUARTER, QUARTER)
+        z1_grp = sbuf("z1_grp", [QUARTER, PACK], BF16, "z0_codes")
+        weave(nc.scalar.copy, z1_grp[:], z1[:])
+        z1_mx = quantize("z1", z1_grp[:].rearrange("p c t -> p (c t)"), QUARTER)
+        z2_grp = sbuf("z2_grp", [QUARTER, PACK], BF16, "z0_1")
+        weave(nc.vector.tensor_copy, z2_grp[:], z2[:])
+        z2_mx = quantize("z2", z2_grp[:].rearrange("p c t -> p (c t)"), QUARTER)
+        leave("res0b", relu_scalar, banks0[1], 2, 2, 0, HALF, 1)
+        close_banks(banks1, z1_mx, QUARTER)
+        close_banks(banks2, z2_mx, QUARTER)
+        for b, relu in enumerate((relu_scalar, relu_vector)):
+            leave("res1_%d" % b, relu, banks1[b], 2 * b, 2, HALF, QUARTER, 2)
+        res2 = sbuf("res2", [PACK, QUARTER], F32)
+        for u, relu in enumerate((relu_scalar, relu_vector) * 2):
+            relu(res2[:, u : u + 1, :], banks2[u][:])
+            if u % 2 == 1:
+                nc.sync.dma_start(out=out_rows[:, u - 1 : u + 1, HALF + QUARTER : S], in_=res2[:, u - 1 : u + 1, :])

@@ -39,21 +39,19 @@ def tile_picked_dmpnn8_relu_p_kernel(
         rev_sb = sbuf("rev_sb", [S // PER_COL], U16)
         words_all = sbuf("words_all", [T], I32)
         scales_all = sbuf("scales_all", [T], U8)
-        w1_raw = [sbuf("w1_raw%d" % h, [2, H], F32) for h in range(2)]
+        w1_raw = sbuf("w1_raw", [PACK, H], F32)
         w2_raw = sbuf("w2_raw", [PACK, N], F32)
         w3_raw = sbuf("w3_raw", [PACK, N], F32)
         y_wide = [sbuf("y_wide%d" % t, [2 * S], F32) for t in range(PACK)]
 
         nc.vector.memset(scales_all[:].bitcast(I32), 0)
-        words_hbm = x_words[0].rearrange("p n t -> p (n t)").bitcast(I32)
-        nc.sync.dma_start(out=words_all[:, 0 : T // 2], in_=words_hbm[:, 0 : T // 2])
+        w1_rows = w1.rearrange("(p j) c -> p j c", j=PACK)
+        nc.sync.dma_start(out=w1_raw[:, 0:2, :], in_=w1_rows[:, 0:2, :])
         nc.sync.dma_start(offs_sb[:], offs)
         for r in range(4):
             nc.sync.dma_start(out=scales_all[r:P:32, :].bitcast(I32), in_=x_scales[0, r:16:4, :].bitcast(I32))
-        nc.sync.dma_start(out=words_all[:, T // 2 : T], in_=words_hbm[:, T // 2 : T])
-        w1_rows = w1.rearrange("(p j) c -> p j c", j=PACK)
-        for h in range(2):
-            nc.sync.dma_start(out=w1_raw[h][:], in_=w1_rows[:, 2 * h : 2 * h + 2, :])
+        nc.sync.dma_start(out=w1_raw[:, 2:4, :], in_=w1_rows[:, 2:4, :])
+        nc.sync.dma_start(out=words_all[:], in_=x_words[0].rearrange("p n t -> p (n t)").bitcast(I32))
         nc.sync.dma_start(rev_sb[:], rev)
         nc.sync.dma_start(in1_sb[:], in1)
         nc.sync.dma_start(in2_sb[:], in2)
@@ -66,7 +64,6 @@ def tile_picked_dmpnn8_relu_p_kernel(
         x_sc = sbuf("x_sc", [S], U8)
         x_q = sbuf("x_q", [S], U32)
         nc.vector.tensor_copy(x_sc[:], scales_all[:].indirect(offs_sb[:]))
-        nc.vector.tensor_copy(x_q[:], words_all[:].bitcast(U32).indirect(offs_sb[:]))
 
         def quantize(name, grouped, width, tag=None):
             codes = sbuf(name + "_codes", [width], U32, tag)
@@ -85,34 +82,34 @@ def tile_picked_dmpnn8_relu_p_kernel(
                 stop=stop,
             )
 
-        plane_sets = ((0, 1), (1, 1), (2, 2))
-        w1_grp = [sbuf("w1_grp%d" % t0, [n, P, PACK], BF16) for t0, n in plane_sets]
+        w1_grp = [sbuf("w1_grp%d" % g, [2, P, PACK], BF16) for g in range(2)]
 
-        def cast_w1(copy, g, h):
-            t0, n = plane_sets[g]
+        def cast_w1(copy, g, j0, j1):
             copy(
-                w1_grp[g][:].rearrange("p t m j -> p m j t")[:, :, 2 * h : 2 * h + 2, :],
-                w1_raw[h][:].rearrange("p j (m t) -> p m j t", t=PACK)[:, :, :, t0 : t0 + n],
+                w1_grp[g][:].rearrange("p t m j -> p m j t")[:, :, j0:j1, :],
+                w1_raw[:].rearrange("p j (m t) -> p m j t", t=PACK)[:, :, j0:j1, 2 * g : 2 * g + 2],
             )
 
-        for g in range(3):
-            cast_w1(nc.scalar.copy, g, 0)
-        cast_w1(nc.vector.tensor_copy, 0, 1)
-        cast_w1(nc.vector.tensor_copy, 1, 1)
-        cast_w1(nc.scalar.copy, 2, 1)
-        w1_mx = [
-            quantize("w1_%d" % g, w1_grp[g][:].rearrange("p t m j -> p (t m j)"), plane_sets[g][1] * P) for g in range(3)
-        ]
+        cast_w1(nc.vector.tensor_copy, 0, 0, 4)
+        cast_w1(nc.scalar.copy, 1, 0, 2)
+        cast_w1(nc.scalar.copy, 1, 2, 4)
+        w1_mx = [quantize("w1_0", w1_grp[0][:].rearrange("p t m j -> p (t m j)"), 2 * P)]
+        for h in range(2):
+            nc.vector.tensor_copy(
+                x_q[:, h * HALF : (h + 1) * HALF],
+                words_all[:].bitcast(U32).indirect(offs_sb[:, h * HALF // PER_COL : (h + 1) * HALF // PER_COL]),
+            )
+        w1_mx.append(quantize("w1_1", w1_grp[1][:].rearrange("p t m j -> p (t m j)"), 2 * P, "words_all"))
         x_mx = (x_q, x_sc)
 
-        for i in range(4):
-            cols = slice(i * QUARTER, (i + 1) * QUARTER)
-            bank = psum.tile([P, QUARTER], F32, name="y0_bank%d" % i, tag="bank%d" % (4 + i))
-            mx(bank[:], w1_mx[0], 0, x_mx, cols, True, True)
-            (nc.vector.tensor_copy, nc.scalar.copy)[i % 2](y_wide[0][:, cols], bank[:])
-        for t, (g, m) in ((1, (1, 0)), (2, (2, 0)), (3, (2, 1))):
+        pieces = ((0, HALF, nc.scalar.copy), (HALF, QUARTER, nc.vector.tensor_copy), (HALF + QUARTER, QUARTER, nc.scalar.copy))
+        for i, (c0, n, copy) in enumerate(pieces):
+            bank = psum.tile([P, n], F32, name="y0_bank%d" % i, tag="bank%d" % (4 + i))
+            mx(bank[:], w1_mx[0], 0, x_mx, slice(c0, c0 + n), True, True)
+            copy(y_wide[0][:, c0 : c0 + n], bank[:])
+        for t in range(1, PACK):
             bank = psum.tile([P, S], F32, name="y_bank%d" % t, tag="bank%d" % t)
-            mx(bank[:], w1_mx[g], m, x_mx, slice(0, S), True, True)
+            mx(bank[:], w1_mx[t // 2], t % 2, x_mx, slice(0, S), True, True)
             nc.scalar.copy(y_wide[t][:, 0:S], bank[:])
 
         def weave(copy, dst, src):
@@ -186,7 +183,6 @@ def tile_picked_dmpnn8_relu_p_kernel(
                 v = (i % 2, i // 2)[b]
                 left, right = ((w2_mx, x_mx), (w3_mx, z0_mx))[second]
                 mx(banks0[b][:, v, :], left, 2 * b + v, right, first, i == 0, i == 3)
-        banks1 = open_banks("o1", ("bank2", "bank3"), HALF, QUARTER)
         banks2 = open_banks("o2", ("bank4", "bank5", "bank6", "bank7"), HALF + QUARTER, QUARTER)
         leave("res0a", relu_scalar, banks0[0], 0, 2, 0, HALF, 1)
 
@@ -203,12 +199,17 @@ def tile_picked_dmpnn8_relu_p_kernel(
         weave(nc.vector.tensor_copy, z2_grp[:], z2[:])
         z2_mx = quantize("z2", z2_grp[:].rearrange("p c t -> p (c t)"), QUARTER)
         leave("res0b", relu_scalar, banks0[1], 2, 2, 0, HALF, 1)
-        close_banks(banks1, z1_mx, QUARTER)
+        banks1 = [psum.tile([P, 2, QUARTER], F32, name="o1_%d" % b, tag="bank%d" % (2 + b)) for b in range(2)]
+        for u in range(PACK):
+            b, v = divmod(u, 2)
+            mx(banks1[b][:, v, :], w3_mx, u, z1_mx, slice(0, QUARTER), True, False)
+            mx(banks1[b][:, v, :], w2_mx, u, x_mx, slice(HALF, HALF + QUARTER), False, True)
         close_banks(banks2, z2_mx, QUARTER)
         for b, relu in enumerate((relu_scalar, relu_vector)):
             leave("res1_%d" % b, relu, banks1[b], 2 * b, 2, HALF, QUARTER, 2)
         res2 = sbuf("res2", [PACK, QUARTER], F32)
         for u, relu in enumerate((relu_scalar, relu_vector) * 2):
             relu(res2[:, u : u + 1, :], banks2[u][:])
-            if u % 2 == 1:
-                nc.sync.dma_start(out=out_rows[:, u - 1 : u + 1, HALF + QUARTER : S], in_=res2[:, u - 1 : u + 1, :])
+            if u >= 1:
+                u0 = (0, 0, 2, 3)[u]
+                nc.sync.dma_start(out=out_rows[:, u0 : u + 1, HALF + QUARTER : S], in_=res2[:, u0 : u + 1, :])

@@ -42,7 +42,7 @@ def tile_picked_dmpnn8_relu_p_kernel(
         w1_raw = sbuf("w1_raw", [PACK, H], F32)
         w2_raw = sbuf("w2_raw", [PACK, N], F32)
         w3_raw = sbuf("w3_raw", [PACK, N], F32)
-        y_wide = [sbuf("y_wide%d" % t, [2 * S], F32) for t in range(PACK)]
+        y = [sbuf("y%d" % t, [2 * S], F32) for t in range(PACK)]
 
         nc.vector.memset(scales_all[:].bitcast(I32), 0)
         w1_rows = w1.rearrange("(p j) c -> p j c", j=PACK)
@@ -59,7 +59,7 @@ def tile_picked_dmpnn8_relu_p_kernel(
             for j in (0, 2):
                 nc.sync.dma_start(out=raw[:, j : j + 2, :], in_=w.rearrange("(p j) c -> p j c", j=PACK)[:, j : j + 2, :])
         for t in range(PACK):
-            nc.vector.memset(y_wide[t][:, S : 2 * S], 0.0)
+            nc.vector.memset(y[t][:, S : 2 * S], 0.0)
 
         x_sc = sbuf("x_sc", [S], U8)
         x_q = sbuf("x_q", [S], U32)
@@ -102,15 +102,19 @@ def tile_picked_dmpnn8_relu_p_kernel(
         w1_mx.append(quantize("w1_1", w1_grp[1][:].rearrange("p t m j -> p (t m j)"), 2 * P, "words_all"))
         x_mx = (x_q, x_sc)
 
-        pieces = ((0, HALF, nc.scalar.copy), (HALF, QUARTER, nc.vector.tensor_copy), (HALF + QUARTER, QUARTER, nc.scalar.copy))
-        for i, (c0, n, copy) in enumerate(pieces):
-            bank = psum.tile([P, n], F32, name="y0_bank%d" % i, tag="bank%d" % (4 + i))
-            mx(bank[:], w1_mx[0], 0, x_mx, slice(c0, c0 + n), True, True)
-            copy(y_wide[0][:, c0 : c0 + n], bank[:])
-        for t in range(1, PACK):
-            bank = psum.tile([P, S], F32, name="y_bank%d" % t, tag="bank%d" % t)
-            mx(bank[:], w1_mx[t // 2], t % 2, x_mx, slice(0, S), True, True)
-            nc.scalar.copy(y_wide[t][:, 0:S], bank[:])
+        pieces = (
+            (0, 0, HALF, nc.scalar.copy),
+            (1, 0, HALF, nc.scalar.copy),
+            (0, HALF, QUARTER, nc.vector.tensor_copy),
+            (0, HALF + QUARTER, QUARTER, nc.scalar.copy),
+            (1, HALF, HALF, nc.scalar.copy),
+            (2, 0, S, nc.scalar.copy),
+            (3, 0, S, nc.scalar.copy),
+        )
+        for i, (t, c0, n, copy) in enumerate(pieces):
+            bank = psum.tile([P, n], F32, name="y_bank%d" % i, tag="bank%d" % i)
+            mx(bank[:], w1_mx[t // 2], t % 2, x_mx, slice(c0, c0 + n), True, True)
+            copy(y[t][:, c0 : c0 + n], bank[:])
 
         def weave(copy, dst, src):
             copy(dst.rearrange("p (c i) t -> p c t i", i=4), src.rearrange("p t (c i) -> p c t i", i=4))
@@ -123,29 +127,38 @@ def tile_picked_dmpnn8_relu_p_kernel(
         w2_mx = weight("w2", w2_raw)
         w3_mx = weight("w3", w3_raw)
 
-        y = [sbuf("y%d" % t, [S], F32) for t in range(PACK)]
-        for t in range(PACK):
-            nc.scalar.copy(y[t][:], y_wide[t][:, 0:S])
+        def entries(tile, c0, n):
+            return tile[:, c0 // PER_COL : (c0 + n) // PER_COL]
 
-        def add_in2(z, windows, part, c0, n):
-            for v in range(2):
-                offsets = in2_sb[:, c0 // PER_COL : (c0 + n) // PER_COL]
-                nc.vector.tensor_tensor(z[:, v, :], windows[v][:].indirect(offsets), part[:, v, c0 : c0 + n], ADD)
+        narrow = [sbuf("narrow%d" % v, [S], F32) for v in range(2)]
+        for v in range(2):
+            nc.scalar.copy(narrow[v][:], y[2 + v][:, 0:S])
 
-        parts = []
-        z0_grp = sbuf("z0_grp", [HALF, PACK], BF16, "w3_raw")
-        for pair in range(2):
-            windows = y_wide[2 * pair : 2 * pair + 2]
-            back = sbuf("back%d" % pair, [2, S], F32, "back")
-            parts.append(sbuf("part%d" % pair, [2, S], F32))
+        def fetch_rev(name, windows, tag):
+            back = sbuf(name, [2, S], F32, tag)
             for v in range(2):
                 nc.vector.tensor_copy(back[:, v, :], windows[v][:].indirect(rev_sb[:]))
+            return back
+
+        def finish(name, windows, back, c0, n, part_tags):
+            part = [sbuf("part%s_%d" % (name, v), [n], F32, part_tags[v]) for v in range(2)]
+            z = sbuf("z" + name, [2, n], F32)
             for v in range(2):
-                nc.vector.tensor_tensor(parts[pair][:, v, :], windows[v][:].indirect(in1_sb[:]), back[:, v, :], SUB)
-            z0 = sbuf("z0_%d" % pair, [2, HALF], F32)
-            add_in2(z0, windows, parts[pair], 0, HALF)
-            weave(nc.scalar.copy, z0_grp[:, :, 2 * pair : 2 * pair + 2], z0[:])
-        z0_mx = quantize("z0", z0_grp[:].rearrange("p c t -> p (c t)"), HALF)
+                nc.vector.tensor_tensor(
+                    part[v][:], windows[v][:].indirect(entries(in1_sb, c0, n)), back[:, v, c0 : c0 + n], SUB
+                )
+            for v in range(2):
+                nc.vector.tensor_tensor(z[:, v, :], windows[v][:].indirect(entries(in2_sb, c0, n)), part[v][:], ADD)
+            return z
+
+        z_low = finish("_low", y[0:2], fetch_rev("back_low", y[0:2], None), 0, S, (None, None))
+        back = fetch_rev("back_high", y[2:4], "back_low")
+        z0 = finish("0", y[2:4], back, 0, HALF, (None, None))
+        grps = [sbuf("z%d_grp" % i, [n, PACK], BF16, ("w3_raw", None, None)[i]) for i, n in enumerate((HALF, QUARTER, QUARTER))]
+        for grp, c0, n in zip(grps, (0, HALF, HALF + QUARTER), (HALF, QUARTER, QUARTER)):
+            weave(nc.scalar.copy, grp[:, :, 0:2], z_low[:, :, c0 : c0 + n])
+        weave(nc.scalar.copy, grps[0][:, :, 2:4], z0[:])
+        z0_mx = quantize("z0", grps[0][:].rearrange("p c t -> p (c t)"), HALF)
 
         out_rows = out.rearrange("(u p) j -> p u j", p=P)
 
@@ -184,21 +197,15 @@ def tile_picked_dmpnn8_relu_p_kernel(
                 left, right = ((w2_mx, x_mx), (w3_mx, z0_mx))[second]
                 mx(banks0[b][:, v, :], left, 2 * b + v, right, first, i == 0, i == 3)
         banks2 = open_banks("o2", ("bank4", "bank5", "bank6", "bank7"), HALF + QUARTER, QUARTER)
-        leave("res0a", relu_scalar, banks0[0], 0, 2, 0, HALF, 1)
 
-        z1 = sbuf("z1", [PACK, QUARTER], F32, "z0_1")
-        for pair in range(2):
-            add_in2(z1[:, 2 * pair : 2 * pair + 2, :], y[2 * pair : 2 * pair + 2], parts[pair], HALF, QUARTER)
-        z2 = sbuf("z2", [PACK, QUARTER], F32, "w3_raw")
-        for pair in range(2):
-            add_in2(z2[:, 2 * pair : 2 * pair + 2, :], y[2 * pair : 2 * pair + 2], parts[pair], HALF + QUARTER, QUARTER)
-        z1_grp = sbuf("z1_grp", [QUARTER, PACK], BF16, "z0_codes")
-        weave(nc.scalar.copy, z1_grp[:], z1[:])
-        z1_mx = quantize("z1", z1_grp[:].rearrange("p c t -> p (c t)"), QUARTER)
-        z2_grp = sbuf("z2_grp", [QUARTER, PACK], BF16, "z0_1")
-        weave(nc.vector.tensor_copy, z2_grp[:], z2[:])
-        z2_mx = quantize("z2", z2_grp[:].rearrange("p c t -> p (c t)"), QUARTER)
-        leave("res0b", relu_scalar, banks0[1], 2, 2, 0, HALF, 1)
+        z1 = finish("1", narrow, back, HALF, QUARTER, ("z0", "w3_raw"))
+        z2 = finish("2", narrow, back, HALF + QUARTER, QUARTER, ("z0", "w3_raw"))
+        weave(nc.scalar.copy, grps[1][:, :, 2:4], z1[:])
+        for b in range(2):
+            leave("res0_%d" % b, relu_scalar, banks0[b], 2 * b, 2, 0, HALF, 1)
+        z1_mx = quantize("z1", grps[1][:].rearrange("p c t -> p (c t)"), QUARTER, "z0")
+        weave(nc.vector.tensor_copy, grps[2][:, :, 2:4], z2[:])
+        z2_mx = quantize("z2", grps[2][:].rearrange("p c t -> p (c t)"), QUARTER)
         banks1 = [psum.tile([P, 2, QUARTER], F32, name="o1_%d" % b, tag="bank%d" % (2 + b)) for b in range(2)]
         for u in range(PACK):
             b, v = divmod(u, 2)

@@ -19,6 +19,7 @@ K, T, S, N, H = 512, 2048, 512, 512, 512
 PER_COL = 16
 HALF = S // 2
 QUARTER = S // 4
+FIRST = HALF + QUARTER
 FLOPS = 2 * S * (K * N + K * H + H * N)
 
 
@@ -42,7 +43,8 @@ def tile_picked_dmpnn8_relu_p_kernel(
         w1_raw = sbuf("w1_raw", [PACK, H], F32)
         w2_raw = sbuf("w2_raw", [PACK, N], F32)
         w3_raw = sbuf("w3_raw", [PACK, N], F32)
-        y = [sbuf("y%d" % t, [2 * S], F32) for t in range(PACK)]
+        widths = (2 * S, 2 * S, 2 * FIRST, 2 * FIRST)
+        y = [sbuf("y%d" % t, [widths[t]], F32) for t in range(PACK)]
 
         nc.vector.memset(scales_all[:].bitcast(I32), 0)
         w1_rows = w1.rearrange("(p j) c -> p j c", j=PACK)
@@ -55,11 +57,11 @@ def tile_picked_dmpnn8_relu_p_kernel(
         nc.sync.dma_start(rev_sb[:], rev)
         nc.sync.dma_start(in1_sb[:], in1)
         nc.sync.dma_start(in2_sb[:], in2)
-        for raw, w in ((w2_raw, w2), (w3_raw, w3)):
-            for j in (0, 2):
-                nc.sync.dma_start(out=raw[:, j : j + 2, :], in_=w.rearrange("(p j) c -> p j c", j=PACK)[:, j : j + 2, :])
+        for j in range(PACK):
+            nc.sync.dma_start(out=w2_raw[:, j, :], in_=w2.rearrange("(p j) c -> p j c", j=PACK)[:, j, :])
+        nc.sync.dma_start(out=w3_raw[:], in_=w3.rearrange("(p j) c -> p j c", j=PACK))
         for t in range(PACK):
-            nc.vector.memset(y[t][:, S : 2 * S], 0.0)
+            nc.vector.memset(y[t][:, S : widths[t]], 0.0)
 
         x_sc = sbuf("x_sc", [S], U8)
         x_q = sbuf("x_q", [S], U32)
@@ -134,46 +136,35 @@ def tile_picked_dmpnn8_relu_p_kernel(
         for v in range(2):
             nc.scalar.copy(narrow[v][:], y[2 + v][:, 0:S])
 
-        def fetch_rev(name, windows, tag):
-            back = sbuf(name, [2, S], F32, tag)
-            for v in range(2):
-                nc.vector.tensor_copy(back[:, v, :], windows[v][:].indirect(rev_sb[:]))
-            return back
-
-        def finish(name, windows, back, c0, n, part_tags):
-            part = [sbuf("part%s_%d" % (name, v), [n], F32, part_tags[v]) for v in range(2)]
+        def gather_run(name, windows, c0, n, first_tag, rest_tag):
+            first = sbuf("first" + name, [n], F32, first_tag)
+            rest = sbuf("rest" + name, [3, n], F32, rest_tag)
             z = sbuf("z" + name, [2, n], F32)
+            back = (first[:], rest[:, 0, :])
             for v in range(2):
-                nc.vector.tensor_tensor(
-                    part[v][:], windows[v][:].indirect(entries(in1_sb, c0, n)), back[:, v, c0 : c0 + n], SUB
-                )
+                nc.vector.tensor_copy(back[v], windows[v][:].indirect(entries(rev_sb, c0, n)))
             for v in range(2):
-                nc.vector.tensor_tensor(z[:, v, :], windows[v][:].indirect(entries(in2_sb, c0, n)), part[v][:], ADD)
+                nc.vector.tensor_tensor(rest[:, 1 + v, :], windows[v][:].indirect(entries(in1_sb, c0, n)), back[v], SUB)
+            for v in range(2):
+                nc.vector.tensor_tensor(z[:, v, :], windows[v][:].indirect(entries(in2_sb, c0, n)), rest[:, 1 + v, :], ADD)
             return z
 
-        z_low = finish("_low", y[0:2], fetch_rev("back_low", y[0:2], None), 0, S, (None, None))
-        back = fetch_rev("back_high", y[2:4], "back_low")
-        z0 = finish("0", y[2:4], back, 0, HALF, (None, None))
-        grps = [sbuf("z%d_grp" % i, [n, PACK], BF16, ("w3_raw", None, None)[i]) for i, n in enumerate((HALF, QUARTER, QUARTER))]
-        for grp, c0, n in zip(grps, (0, HALF, HALF + QUARTER), (HALF, QUARTER, QUARTER)):
-            weave(nc.scalar.copy, grp[:, :, 0:2], z_low[:, :, c0 : c0 + n])
-        weave(nc.scalar.copy, grps[0][:, :, 2:4], z0[:])
-        z0_mx = quantize("z0", grps[0][:].rearrange("p c t -> p (c t)"), HALF)
+        spans = ((0, HALF), (HALF, QUARTER), (FIRST, QUARTER))
+        z_low = gather_run("_low", y[0:2], 0, S, None, None)
+        z_high = gather_run("_high", y[2:4], 0, FIRST, "first_low", None)
+        z_grp = sbuf("z_grp", [S, PACK], BF16, "w3_raw")
+        weave(nc.scalar.copy, z_grp[:, :, 0:2], z_low[:])
+
+        def quantize_z(i, copy, planes):
+            c0, n = spans[i]
+            weave(copy, z_grp[:, c0 : c0 + n, 2:4], planes)
+            return quantize("z%d" % i, z_grp[:, c0 : c0 + n, :].rearrange("p c t -> p (c t)"), n)
+
+        z_mx = [quantize_z(0, nc.scalar.copy, z_high[:, :, 0:HALF]), quantize_z(1, nc.scalar.copy, z_high[:, :, HALF:FIRST])]
+        z_last = gather_run("_last", narrow, FIRST, QUARTER, "w3_grp", "z_high")
+        z_mx.append(quantize_z(2, nc.vector.tensor_copy, z_last[:]))
 
         out_rows = out.rearrange("(u p) j -> p u j", p=P)
-
-        def open_banks(name, tags, c0, n):
-            per_bank = PACK // len(tags)
-            banks = [psum.tile([P, per_bank, n], F32, name="%s_%d" % (name, b), tag=tag) for b, tag in enumerate(tags)]
-            for u in range(PACK):
-                mx(banks[u // per_bank][:, u % per_bank, :], w2_mx, u, x_mx, slice(c0, c0 + n), u % per_bank == 0, False)
-            return banks
-
-        def close_banks(banks, z_mx, n):
-            per_bank = PACK // len(banks)
-            for u in range(PACK):
-                b, v = divmod(u, per_bank)
-                mx(banks[b][:, v, :], w3_mx, u, z_mx, slice(0, n), False, v == per_bank - 1)
 
         def relu_scalar(dst, src):
             nc.scalar.activation(dst, src, RELU)
@@ -181,42 +172,32 @@ def tile_picked_dmpnn8_relu_p_kernel(
         def relu_vector(dst, src):
             nc.vector.tensor_scalar_max(dst, src, 0.0)
 
-        def leave(name, relu, bank, u0, rows, c0, n, per_store, tag=None):
-            res = sbuf(name, [rows, n], F32, tag)
-            relu(res[:], bank[:])
-            for v in range(0, rows, per_store):
-                nc.sync.dma_start(
-                    out=out_rows[:, u0 + v : u0 + v + per_store, c0 : c0 + n], in_=res[:, v : v + per_store, :]
-                )
+        def products(name, parts, relus, tags, ahead):
+            base = spans[parts[0]][0]
+            width = sum(spans[i][1] for i in parts)
+            banks = [psum.tile([P, width], F32, name="%s_bank%d" % (name, u), tag="bank%d" % tags[u]) for u in range(PACK)]
+            res = sbuf(name, [PACK, width], F32)
 
-        banks0 = [psum.tile([P, 2, HALF], F32, name="o0_%d" % b, tag="bank%d" % b) for b in range(2)]
-        first = slice(0, HALF)
-        for b, order in enumerate(((0, 0, 1, 1), (1, 0, 1, 0))):
-            for i, second in enumerate(order):
-                v = (i % 2, i // 2)[b]
-                left, right = ((w2_mx, x_mx), (w3_mx, z0_mx))[second]
-                mx(banks0[b][:, v, :], left, 2 * b + v, right, first, i == 0, i == 3)
-        banks2 = open_banks("o2", ("bank4", "bank5", "bank6", "bank7"), HALF + QUARTER, QUARTER)
+            def h0_passes(u, start, stop):
+                for i in parts:
+                    c0, n = spans[i]
+                    dst = banks[u][:, c0 - base : c0 - base + n]
+                    mx(dst, w2_mx, u, x_mx, slice(c0, c0 + n), start and i == parts[0], stop and i == parts[-1])
 
-        z1 = finish("1", narrow, back, HALF, QUARTER, ("z0", "w3_raw"))
-        z2 = finish("2", narrow, back, HALF + QUARTER, QUARTER, ("z0", "w3_raw"))
-        weave(nc.scalar.copy, grps[1][:, :, 2:4], z1[:])
-        for b in range(2):
-            leave("res0_%d" % b, relu_scalar, banks0[b], 2 * b, 2, 0, HALF, 1)
-        z1_mx = quantize("z1", grps[1][:].rearrange("p c t -> p (c t)"), QUARTER, "z0")
-        weave(nc.vector.tensor_copy, grps[2][:, :, 2:4], z2[:])
-        z2_mx = quantize("z2", grps[2][:].rearrange("p c t -> p (c t)"), QUARTER)
-        banks1 = [psum.tile([P, 2, QUARTER], F32, name="o1_%d" % b, tag="bank%d" % (2 + b)) for b in range(2)]
-        for u in range(PACK):
-            b, v = divmod(u, 2)
-            mx(banks1[b][:, v, :], w3_mx, u, z1_mx, slice(0, QUARTER), True, False)
-            mx(banks1[b][:, v, :], w2_mx, u, x_mx, slice(HALF, HALF + QUARTER), False, True)
-        close_banks(banks2, z2_mx, QUARTER)
-        for b, relu in enumerate((relu_scalar, relu_vector)):
-            leave("res1_%d" % b, relu, banks1[b], 2 * b, 2, HALF, QUARTER, 2)
-        res2 = sbuf("res2", [PACK, QUARTER], F32)
-        for u, relu in enumerate((relu_scalar, relu_vector) * 2):
-            relu(res2[:, u : u + 1, :], banks2[u][:])
-            if u >= 1:
-                u0 = (0, 0, 2, 3)[u]
-                nc.sync.dma_start(out=out_rows[:, u0 : u + 1, HALF + QUARTER : S], in_=res2[:, u0 : u + 1, :])
+            def z_passes(u, start, stop):
+                for i in parts:
+                    c0, n = spans[i]
+                    dst = banks[u][:, c0 - base : c0 - base + n]
+                    mx(dst, w3_mx, u, z_mx[i], slice(0, n), start and i == parts[0], stop and i == parts[-1])
+
+            for u in range(ahead):
+                h0_passes(u, True, False)
+            for u in range(PACK):
+                z_passes(u, u >= ahead, u < ahead)
+                if u >= ahead:
+                    h0_passes(u, False, True)
+                relus[u](res[:, u, :], banks[u][:])
+                nc.sync.dma_start(out=out_rows[:, u, base : base + width], in_=res[:, u, :])
+
+        products("res_first", (0, 1), (relu_scalar,) * 4, (0, 1, 2, 3), 2)
+        products("res_last", (2,), (relu_scalar, relu_vector) * 2, (0, 1, 4, 5), 4)

@@ -41,8 +41,6 @@ def tile_picked_dmpnn8_relu_p_kernel(
         words_all = sbuf("words_all", [T], I32)
         scales_all = sbuf("scales_all", [T], U8)
         w1_raw = sbuf("w1_raw", [PACK, H], F32)
-        w2_raw = sbuf("w2_raw", [PACK, N], F32)
-        w3_raw = sbuf("w3_raw", [PACK, N], F32)
         widths = (2 * S, 2 * S, 2 * FIRST, 2 * FIRST)
         y = [sbuf("y%d" % t, [widths[t]], F32) for t in range(PACK)]
 
@@ -50,22 +48,26 @@ def tile_picked_dmpnn8_relu_p_kernel(
         w1_rows = w1.rearrange("(p j) c -> p j c", j=PACK)
         nc.sync.dma_start(out=w1_raw[:, 0:2, :], in_=w1_rows[:, 0:2, :])
         nc.sync.dma_start(offs_sb[:], offs)
-        for r in range(4):
-            nc.sync.dma_start(out=scales_all[r:P:32, :].bitcast(I32), in_=x_scales[0, r:16:4, :].bitcast(I32))
+        nc.sync.dma_start(out=scales_all[0:P:8, :].bitcast(I32), in_=x_scales[0].bitcast(I32))
         nc.sync.dma_start(out=w1_raw[:, 2:4, :], in_=w1_rows[:, 2:4, :])
         nc.sync.dma_start(out=words_all[:], in_=x_words[0].rearrange("p n t -> p (n t)").bitcast(I32))
         nc.sync.dma_start(rev_sb[:], rev)
         nc.sync.dma_start(in1_sb[:], in1)
         nc.sync.dma_start(in2_sb[:], in2)
-        for j in range(PACK):
-            nc.sync.dma_start(out=w2_raw[:, j, :], in_=w2.rearrange("(p j) c -> p j c", j=PACK)[:, j, :])
-        nc.sync.dma_start(out=w3_raw[:], in_=w3.rearrange("(p j) c -> p j c", j=PACK))
         for t in range(PACK):
             nc.vector.memset(y[t][:, S : widths[t]], 0.0)
 
         x_sc = sbuf("x_sc", [S], U8)
+        nc.vector.memset(x_sc[:].bitcast(I32), 0)
         x_q = sbuf("x_q", [S], U32)
-        nc.vector.tensor_copy(x_sc[:], scales_all[:].indirect(offs_sb[:]))
+        picked_sc = sbuf("picked_sc", [S], U8)
+        nc.vector.tensor_copy(picked_sc[:], scales_all[:].indirect(offs_sb[:]))
+        for r in range(4):
+            nc.sync.dma_start(out=x_sc[r:P:32, :].bitcast(I32), in_=picked_sc[8 * r : P : 32, :].bitcast(I32))
+        w23_raw = sbuf("w23_raw", [2, PACK, N], F32, "scales_all")
+        for i, w in enumerate((w2, w3)):
+            for j in (0, 2):
+                nc.sync.dma_start(out=w23_raw[:, i, j : j + 2, :], in_=w.rearrange("(p j) c -> p j c", j=PACK)[:, j : j + 2, :])
 
         def quantize(name, grouped, width, tag=None):
             codes = sbuf(name + "_codes", [width], U32, tag)
@@ -123,11 +125,11 @@ def tile_picked_dmpnn8_relu_p_kernel(
 
         def weight(name, raw):
             grp = sbuf(name + "_grp", [N, PACK], BF16)
-            weave(nc.scalar.copy, grp[:], raw[:])
-            return quantize(name, grp[:].rearrange("p c j -> p (c j)"), N)
+            weave(nc.scalar.copy, grp[:], raw)
+            return grp[:].rearrange("p c j -> p (c j)")
 
-        w2_mx = weight("w2", w2_raw)
-        w3_mx = weight("w3", w3_raw)
+        w2_grp = weight("w2", w23_raw[:, 0])
+        w3_grp = weight("w3", w23_raw[:, 1])
 
         def entries(tile, c0, n):
             return tile[:, c0 // PER_COL : (c0 + n) // PER_COL]
@@ -152,7 +154,9 @@ def tile_picked_dmpnn8_relu_p_kernel(
         spans = ((0, HALF), (HALF, QUARTER), (FIRST, QUARTER))
         z_low = gather_run("_low", y[0:2], 0, S, None, None)
         z_high = gather_run("_high", y[2:4], 0, FIRST, "first_low", None)
-        z_grp = sbuf("z_grp", [S, PACK], BF16, "w3_raw")
+        w2_mx = quantize("w2", w2_grp, N, "first_low")
+        w3_mx = quantize("w3", w3_grp, N)
+        z_grp = sbuf("z_grp", [S, PACK], BF16, "scales_all")
         weave(nc.scalar.copy, z_grp[:, :, 0:2], z_low[:])
 
         def quantize_z(i, copy, planes):

@@ -165,7 +165,7 @@ def tile_picked_dmpnn8_relu_p_kernel(
             return quantize("z%d" % i, z_grp[:, c0 : c0 + n, :].rearrange("p c t -> p (c t)"), n)
 
         z_mx = [quantize_z(0, nc.scalar.copy, z_high[:, :, 0:HALF]), quantize_z(1, nc.scalar.copy, z_high[:, :, HALF:FIRST])]
-        z_last = gather_run("_last", narrow, FIRST, QUARTER, "w3_grp", "z_high")
+        z_last = gather_run("_last", narrow, FIRST, QUARTER, "z_low", "z_high")
         z_mx.append(quantize_z(2, nc.vector.tensor_copy, z_last[:]))
 
         out_rows = out.rearrange("(u p) j -> p u j", p=P)

@@ -63,7 +63,7 @@ def tile_picked_dmpnn8_relu_p_kernel(
         picked_sc = sbuf("picked_sc", [S], U8)
         nc.vector.tensor_copy(picked_sc[:], scales_all[:].indirect(offs_sb[:]))
         for r in range(4):
-            nc.sync.dma_start(out=x_sc[r:P:32, :].bitcast(I32), in_=picked_sc[8 * r : P : 32, :].bitcast(I32))
+            nc.scalar.dma_start(out=x_sc[r:P:32, :].bitcast(I32), in_=picked_sc[8 * r : P : 32, :].bitcast(I32))
         w23_raw = sbuf("w23_raw", [2, PACK, N], F32, "scales_all")
         for i, w in enumerate((w2, w3)):
             for j in (0, 2):

@@ -40,17 +40,19 @@ def tile_picked_dmpnn8_relu_p_kernel(
         rev_sb = sbuf("rev_sb", [S // PER_COL], U16)
         words_all = sbuf("words_all", [T], I32)
         scales_all = sbuf("scales_all", [T], U8)
-        w1_raw = sbuf("w1_raw", [PACK, H], F32)
+        w1_raw = [sbuf("w1_raw%d" % h, [2, H], F32) for h in range(2)]
         widths = (2 * S, 2 * S, 2 * FIRST, 2 * FIRST)
         y = [sbuf("y%d" % t, [widths[t]], F32) for t in range(PACK)]
 
         nc.vector.memset(scales_all[:].bitcast(I32), 0)
         w1_rows = w1.rearrange("(p j) c -> p j c", j=PACK)
-        nc.sync.dma_start(out=w1_raw[:, 0:2, :], in_=w1_rows[:, 0:2, :])
+        x_rows = x_words[0].rearrange("p n t -> p (n t)").bitcast(I32)
+        nc.sync.dma_start(out=words_all[:, 0 : T // 2], in_=x_rows[:, 0 : T // 2])
         nc.sync.dma_start(offs_sb[:], offs)
         nc.sync.dma_start(out=scales_all[0:P:8, :].bitcast(I32), in_=x_scales[0].bitcast(I32))
-        nc.sync.dma_start(out=w1_raw[:, 2:4, :], in_=w1_rows[:, 2:4, :])
-        nc.sync.dma_start(out=words_all[:], in_=x_words[0].rearrange("p n t -> p (n t)").bitcast(I32))
+        nc.sync.dma_start(out=words_all[:, T // 2 : T], in_=x_rows[:, T // 2 : T])
+        for h in range(2):
+            nc.sync.dma_start(out=w1_raw[h][:], in_=w1_rows[:, 2 * h : 2 * h + 2, :])
         nc.sync.dma_start(rev_sb[:], rev)
         nc.sync.dma_start(in1_sb[:], in1)
         nc.sync.dma_start(in2_sb[:], in2)
@@ -63,11 +65,13 @@ def tile_picked_dmpnn8_relu_p_kernel(
         picked_sc = sbuf("picked_sc", [S], U8)
         nc.vector.tensor_copy(picked_sc[:], scales_all[:].indirect(offs_sb[:]))
         for r in range(4):
-            nc.scalar.dma_start(out=x_sc[r:P:32, :].bitcast(I32), in_=picked_sc[8 * r : P : 32, :].bitcast(I32))
+            nc.sync.dma_start(out=x_sc[r:P:32, :].bitcast(I32), in_=picked_sc[8 * r : P : 32, :].bitcast(I32))
+        nc.vector.tensor_copy(x_q[:], words_all[:].bitcast(U32).indirect(offs_sb[:]))
+        x_mx = (x_q, x_sc)
         w23_raw = sbuf("w23_raw", [2, PACK, N], F32, "scales_all")
-        for i, w in enumerate((w2, w3)):
-            for j in (0, 2):
-                nc.sync.dma_start(out=w23_raw[:, i, j : j + 2, :], in_=w.rearrange("(p j) c -> p j c", j=PACK)[:, j : j + 2, :])
+        nc.sync.dma_start(out=w23_raw[:, 0], in_=w2.rearrange("(p j) c -> p j c", j=PACK))
+        for j in (0, 2):
+            nc.sync.dma_start(out=w23_raw[:, 1, j : j + 2, :], in_=w3.rearrange("(p j) c -> p j c", j=PACK)[:, j : j + 2, :])
 
         def quantize(name, grouped, width, tag=None):
             codes = sbuf(name + "_codes", [width], U32, tag)
@@ -88,36 +92,27 @@ def tile_picked_dmpnn8_relu_p_kernel(
 
         w1_grp = [sbuf("w1_grp%d" % g, [2, P, PACK], BF16) for g in range(2)]
 
-        def cast_w1(copy, g, j0, j1):
+        def cast_w1(copy, h, t0, t1):
             copy(
-                w1_grp[g][:].rearrange("p t m j -> p m j t")[:, :, j0:j1, :],
-                w1_raw[:].rearrange("p j (m t) -> p m j t", t=PACK)[:, :, j0:j1, 2 * g : 2 * g + 2],
+                w1_grp[t0 // 2][:].rearrange("p t m j -> p m j t")[:, :, 2 * h : 2 * h + 2, t0 % 2 : t0 % 2 + t1 - t0],
+                w1_raw[h][:].rearrange("p j (m t) -> p m j t", t=PACK)[:, :, :, t0:t1],
             )
 
-        cast_w1(nc.vector.tensor_copy, 0, 0, 4)
-        cast_w1(nc.scalar.copy, 1, 0, 2)
+        cast_w1(nc.vector.tensor_copy, 0, 0, 2)
+        cast_w1(nc.scalar.copy, 0, 2, 4)
+        cast_w1(nc.vector.tensor_copy, 1, 0, 1)
+        cast_w1(nc.vector.tensor_copy, 1, 1, 2)
         cast_w1(nc.scalar.copy, 1, 2, 4)
-        w1_mx = [quantize("w1_0", w1_grp[0][:].rearrange("p t m j -> p (t m j)"), 2 * P)]
-        for h in range(2):
-            nc.vector.tensor_copy(
-                x_q[:, h * HALF : (h + 1) * HALF],
-                words_all[:].bitcast(U32).indirect(offs_sb[:, h * HALF // PER_COL : (h + 1) * HALF // PER_COL]),
-            )
-        w1_mx.append(quantize("w1_1", w1_grp[1][:].rearrange("p t m j -> p (t m j)"), 2 * P, "words_all"))
-        x_mx = (x_q, x_sc)
+        w1_low = [quantize("w1_%d" % t, w1_grp[0][:, t].rearrange("p m j -> p (m j)"), P) for t in range(2)]
+        w1_high = quantize("w1_high", w1_grp[1][:].rearrange("p t m j -> p (t m j)"), 2 * P)
+        w1_mx = ((w1_low[0], 0), (w1_low[1], 0), (w1_high, 0), (w1_high, 1))
 
-        pieces = (
-            (0, 0, HALF, nc.scalar.copy),
-            (1, 0, HALF, nc.scalar.copy),
-            (0, HALF, QUARTER, nc.vector.tensor_copy),
-            (0, HALF + QUARTER, QUARTER, nc.scalar.copy),
-            (1, HALF, HALF, nc.scalar.copy),
-            (2, 0, S, nc.scalar.copy),
-            (3, 0, S, nc.scalar.copy),
-        )
+        pieces = [(0, q * QUARTER, QUARTER, (nc.vector.tensor_copy, nc.scalar.copy)[q % 2]) for q in range(4)]
+        pieces += [(1, h * HALF, HALF, nc.scalar.copy) for h in range(2)]
+        pieces += [(t, 0, S, nc.scalar.copy) for t in (2, 3)]
         for i, (t, c0, n, copy) in enumerate(pieces):
-            bank = psum.tile([P, n], F32, name="y_bank%d" % i, tag="bank%d" % i)
-            mx(bank[:], w1_mx[t // 2], t % 2, x_mx, slice(c0, c0 + n), True, True)
+            bank = psum.tile([P, n], F32, name="y_bank%d" % i, tag="bank%d" % (0, 1, 2, 3, 4, 5, 5, 6)[i])
+            mx(bank[:], w1_mx[t][0], w1_mx[t][1], x_mx, slice(c0, c0 + n), True, True)
             copy(y[t][:, c0 : c0 + n], bank[:])
 
         def weave(copy, dst, src):
@@ -138,22 +133,24 @@ def tile_picked_dmpnn8_relu_p_kernel(
         for v in range(2):
             nc.scalar.copy(narrow[v][:], y[2 + v][:, 0:S])
 
-        def gather_run(name, windows, c0, n, first_tag, rest_tag):
-            first = sbuf("first" + name, [n], F32, first_tag)
-            rest = sbuf("rest" + name, [3, n], F32, rest_tag)
+        def gather_run(name, windows, c0, n, back, part):
             z = sbuf("z" + name, [2, n], F32)
-            back = (first[:], rest[:, 0, :])
             for v in range(2):
                 nc.vector.tensor_copy(back[v], windows[v][:].indirect(entries(rev_sb, c0, n)))
             for v in range(2):
-                nc.vector.tensor_tensor(rest[:, 1 + v, :], windows[v][:].indirect(entries(in1_sb, c0, n)), back[v], SUB)
+                nc.vector.tensor_tensor(part[v], windows[v][:].indirect(entries(in1_sb, c0, n)), back[v], SUB)
             for v in range(2):
-                nc.vector.tensor_tensor(z[:, v, :], windows[v][:].indirect(entries(in2_sb, c0, n)), rest[:, 1 + v, :], ADD)
+                nc.vector.tensor_tensor(z[:, v, :], windows[v][:].indirect(entries(in2_sb, c0, n)), part[v], ADD)
             return z
 
+        def rows(name, count, n, tag=None):
+            tile = sbuf(name, [count, n], F32, tag)
+            return [tile[:, v, :] for v in range(count)]
+
         spans = ((0, HALF), (HALF, QUARTER), (FIRST, QUARTER))
-        z_low = gather_run("_low", y[0:2], 0, S, None, None)
-        z_high = gather_run("_high", y[2:4], 0, FIRST, "first_low", None)
+        z_low = gather_run("_low", y[0:2], 0, S, rows("first_low", 1, S) + rows("second_low", 1, S), rows("part_low", 2, S, "w1_high_codes"))
+        high = rows("first_high", 1, FIRST, "first_low") + rows("rest_high", 3, FIRST)
+        z_high = gather_run("_high", y[2:4], 0, FIRST, high[0:2], high[2:4])
         w2_mx = quantize("w2", w2_grp, N, "first_low")
         w3_mx = quantize("w3", w3_grp, N)
         z_grp = sbuf("z_grp", [S, PACK], BF16, "scales_all")
@@ -165,7 +162,8 @@ def tile_picked_dmpnn8_relu_p_kernel(
             return quantize("z%d" % i, z_grp[:, c0 : c0 + n, :].rearrange("p c t -> p (c t)"), n)
 
         z_mx = [quantize_z(0, nc.scalar.copy, z_high[:, :, 0:HALF]), quantize_z(1, nc.scalar.copy, z_high[:, :, HALF:FIRST])]
-        z_last = gather_run("_last", narrow, FIRST, QUARTER, "z_low", "z_high")
+        last = rows("first_last", 1, QUARTER, "z_low") + rows("rest_last", 3, QUARTER, "z_high")
+        z_last = gather_run("_last", narrow, FIRST, QUARTER, last[0:2], last[2:4])
         z_mx.append(quantize_z(2, nc.vector.tensor_copy, z_last[:]))
 
         out_rows = out.rearrange("(u p) j -> p u j", p=P)

@@ -40,7 +40,7 @@ def tile_picked_dmpnn8_relu_p_kernel(
         rev_sb = sbuf("rev_sb", [S // PER_COL], U16)
         words_all = sbuf("words_all", [T], I32)
         scales_all = sbuf("scales_all", [T], U8)
-        w1_raw = [sbuf("w1_raw%d" % h, [2, H], F32) for h in range(2)]
+        w1_raw = sbuf("w1_raw", [PACK, H], F32)
         widths = (2 * S, 2 * S, 2 * FIRST, 2 * FIRST)
         y = [sbuf("y%d" % t, [widths[t]], F32) for t in range(PACK)]
 
@@ -51,8 +51,7 @@ def tile_picked_dmpnn8_relu_p_kernel(
         nc.sync.dma_start(offs_sb[:], offs)
         nc.sync.dma_start(out=scales_all[0:P:8, :].bitcast(I32), in_=x_scales[0].bitcast(I32))
         nc.sync.dma_start(out=words_all[:, T // 2 : T], in_=x_rows[:, T // 2 : T])
-        for h in range(2):
-            nc.sync.dma_start(out=w1_raw[h][:], in_=w1_rows[:, 2 * h : 2 * h + 2, :])
+        nc.sync.dma_start(out=w1_raw[:], in_=w1_rows)
         nc.sync.dma_start(rev_sb[:], rev)
         nc.sync.dma_start(in1_sb[:], in1)
         nc.sync.dma_start(in2_sb[:], in2)
@@ -69,9 +68,11 @@ def tile_picked_dmpnn8_relu_p_kernel(
         nc.vector.tensor_copy(x_q[:], words_all[:].bitcast(U32).indirect(offs_sb[:]))
         x_mx = (x_q, x_sc)
         w23_raw = sbuf("w23_raw", [2, PACK, N], F32, "scales_all")
-        nc.sync.dma_start(out=w23_raw[:, 0], in_=w2.rearrange("(p j) c -> p j c", j=PACK))
-        for j in (0, 2):
-            nc.sync.dma_start(out=w23_raw[:, 1, j : j + 2, :], in_=w3.rearrange("(p j) c -> p j c", j=PACK)[:, j : j + 2, :])
+        for j in range(PACK):
+            nc.sync.dma_start(out=w23_raw[:, 0, j, :], in_=w2.rearrange("(p j) c -> p j c", j=PACK)[:, j, :])
+        w3_rows = w3.rearrange("(b t q) c -> q b t c", t=PACK, q=8)
+        for q in range(8):
+            nc.sync.dma_start(out=w23_raw[q:P:8, 1], in_=w3_rows[q])
 
         def quantize(name, grouped, width, tag=None):
             codes = sbuf(name + "_codes", [width], U32, tag)
@@ -90,30 +91,33 @@ def tile_picked_dmpnn8_relu_p_kernel(
                 stop=stop,
             )
 
-        w1_grp = [sbuf("w1_grp%d" % g, [2, P, PACK], BF16) for g in range(2)]
+        w1_grp = [sbuf("w1_grp%d" % t, [P, PACK], BF16) for t in range(PACK)]
+        w1_cols = w1_raw[:].rearrange("p j (b t h i) -> p t b h j i", t=PACK, h=2, i=4)
 
-        def cast_w1(copy, h, t0, t1):
-            copy(
-                w1_grp[t0 // 2][:].rearrange("p t m j -> p m j t")[:, :, 2 * h : 2 * h + 2, t0 % 2 : t0 % 2 + t1 - t0],
-                w1_raw[h][:].rearrange("p j (m t) -> p m j t", t=PACK)[:, :, :, t0:t1],
-            )
+        def cast_w1(copy, t):
+            copy(w1_grp[t][:].rearrange("p (b h i) j -> p b h j i", h=2, i=4), w1_cols[:, t])
 
-        cast_w1(nc.vector.tensor_copy, 0, 0, 2)
-        cast_w1(nc.scalar.copy, 0, 2, 4)
-        cast_w1(nc.vector.tensor_copy, 1, 0, 1)
-        cast_w1(nc.vector.tensor_copy, 1, 1, 2)
-        cast_w1(nc.scalar.copy, 1, 2, 4)
-        w1_low = [quantize("w1_%d" % t, w1_grp[0][:, t].rearrange("p m j -> p (m j)"), P) for t in range(2)]
-        w1_high = quantize("w1_high", w1_grp[1][:].rearrange("p t m j -> p (t m j)"), 2 * P)
-        w1_mx = ((w1_low[0], 0), (w1_low[1], 0), (w1_high, 0), (w1_high, 1))
+        def quantize_w1(t, tag=None):
+            return quantize("w1_%d" % t, w1_grp[t][:].rearrange("p m j -> p (m j)"), P, tag)
 
-        pieces = [(0, q * QUARTER, QUARTER, (nc.vector.tensor_copy, nc.scalar.copy)[q % 2]) for q in range(4)]
-        pieces += [(1, h * HALF, HALF, nc.scalar.copy) for h in range(2)]
-        pieces += [(t, 0, S, nc.scalar.copy) for t in (2, 3)]
-        for i, (t, c0, n, copy) in enumerate(pieces):
-            bank = psum.tile([P, n], F32, name="y_bank%d" % i, tag="bank%d" % (0, 1, 2, 3, 4, 5, 5, 6)[i])
-            mx(bank[:], w1_mx[t][0], w1_mx[t][1], x_mx, slice(c0, c0 + n), True, True)
+        def y_piece(i, t, c0, n, codes, copy):
+            bank = psum.tile([P, n], F32, name="y%d_%d" % (t, c0), tag="bank%d" % i)
+            mx(bank[:], codes, 0, x_mx, slice(c0, c0 + n), True, True)
             copy(y[t][:, c0 : c0 + n], bank[:])
+
+        cast_w1(nc.scalar.copy, 3)
+        cast_w1(nc.vector.tensor_copy, 0)
+        cast_w1(nc.vector.tensor_copy, 1)
+        w1_mx = {t: quantize_w1(t) for t in (0, 1)}
+        cast_w1(nc.vector.tensor_copy, 2)
+        w1_mx.update({3: quantize_w1(3)})
+        for q in range(4):
+            y_piece(q, 0, q * QUARTER, QUARTER, w1_mx[0], (nc.vector.tensor_copy, nc.scalar.copy)[q % 2])
+        w1_mx.update({2: quantize_w1(2, "w1_0_codes")})
+        for h in range(2):
+            y_piece(4 + h, 1, h * HALF, HALF, w1_mx[1], nc.scalar.copy)
+        y_piece(6, 2, 0, S, w1_mx[2], nc.scalar.copy)
+        y_piece(5, 3, 0, S, w1_mx[3], nc.scalar.copy)
 
         def weave(copy, dst, src):
             copy(dst.rearrange("p (c i) t -> p c t i", i=4), src.rearrange("p t (c i) -> p c t i", i=4))
@@ -148,7 +152,7 @@ def tile_picked_dmpnn8_relu_p_kernel(
             return [tile[:, v, :] for v in range(count)]
 
         spans = ((0, HALF), (HALF, QUARTER), (FIRST, QUARTER))
-        z_low = gather_run("_low", y[0:2], 0, S, rows("first_low", 1, S) + rows("second_low", 1, S), rows("part_low", 2, S, "w1_high_codes"))
+        z_low = gather_run("_low", y[0:2], 0, S, rows("first_low", 1, S) + rows("second_low", 1, S), rows("part_low", 2, S, "w1_3_codes"))
         high = rows("first_high", 1, FIRST, "first_low") + rows("rest_high", 3, FIRST)
         z_high = gather_run("_high", y[2:4], 0, FIRST, high[0:2], high[2:4])
         w2_mx = quantize("w2", w2_grp, N, "first_low")

@@ -68,11 +68,10 @@ def tile_picked_dmpnn8_relu_p_kernel(
         nc.vector.tensor_copy(x_q[:], words_all[:].bitcast(U32).indirect(offs_sb[:]))
         x_mx = (x_q, x_sc)
         w23_raw = sbuf("w23_raw", [2, PACK, N], F32, "scales_all")
-        for j in range(PACK):
-            nc.sync.dma_start(out=w23_raw[:, 0, j, :], in_=w2.rearrange("(p j) c -> p j c", j=PACK)[:, j, :])
-        w3_rows = w3.rearrange("(b t q) c -> q b t c", t=PACK, q=8)
-        for q in range(8):
-            nc.sync.dma_start(out=w23_raw[q:P:8, 1], in_=w3_rows[q])
+        nc.sync.dma_start(out=w23_raw[:, 0], in_=w2.rearrange("(p j) c -> p j c", j=PACK))
+        w3_rows = w3.rearrange("(g t i) c -> i g t c", t=PACK, i=4)
+        for i in range(4):
+            nc.sync.dma_start(out=w23_raw[i:P:4, 1], in_=w3_rows[i])
 
         def quantize(name, grouped, width, tag=None):
             codes = sbuf(name + "_codes", [width], U32, tag)
@@ -92,10 +91,10 @@ def tile_picked_dmpnn8_relu_p_kernel(
             )
 
         w1_grp = [sbuf("w1_grp%d" % t, [P, PACK], BF16) for t in range(PACK)]
-        w1_cols = w1_raw[:].rearrange("p j (b t h i) -> p t b h j i", t=PACK, h=2, i=4)
+        w1_cols = w1_raw[:].rearrange("p j (g t i) -> p t g i j", t=PACK, i=4)
 
         def cast_w1(copy, t):
-            copy(w1_grp[t][:].rearrange("p (b h i) j -> p b h j i", h=2, i=4), w1_cols[:, t])
+            copy(w1_grp[t][:].rearrange("p (g i) j -> p g i j", i=4), w1_cols[:, t])
 
         def quantize_w1(t, tag=None):
             return quantize("w1_%d" % t, w1_grp[t][:].rearrange("p m j -> p (m j)"), P, tag)
@@ -178,7 +177,7 @@ def tile_picked_dmpnn8_relu_p_kernel(
         def relu_vector(dst, src):
             nc.vector.tensor_scalar_max(dst, src, 0.0)
 
-        def products(name, parts, relus, tags, ahead):
+        def products(name, parts, relus, tags, ahead, stores):
             base = spans[parts[0]][0]
             width = sum(spans[i][1] for i in parts)
             banks = [psum.tile([P, width], F32, name="%s_bank%d" % (name, u), tag="bank%d" % tags[u]) for u in range(PACK)]
@@ -203,7 +202,9 @@ def tile_picked_dmpnn8_relu_p_kernel(
                 if u >= ahead:
                     h0_passes(u, False, True)
                 relus[u](res[:, u, :], banks[u][:])
-                nc.sync.dma_start(out=out_rows[:, u, base : base + width], in_=res[:, u, :])
+                if u in stores:
+                    rows_out = slice(stores[u], u + 1)
+                    nc.sync.dma_start(out=out_rows[:, rows_out, base : base + width], in_=res[:, rows_out, :])
 
-        products("res_first", (0, 1), (relu_scalar,) * 4, (0, 1, 2, 3), 2)
-        products("res_last", (2,), (relu_scalar, relu_vector) * 2, (0, 1, 4, 5), 4)
+        products("res_first", (0, 1), (relu_scalar,) * 4, (0, 1, 2, 3), 2, {0: 0, 1: 1, 2: 2, 3: 3})
+        products("res_last", (2,), (relu_scalar, relu_vector) * 2, (0, 1, 4, 5), 4, {0: 0, 1: 1, 3: 2})

@@ -90,6 +90,10 @@ def tile_picked_dmpnn8_relu_p_kernel(
                 stop=stop,
             )
 
+        warm = psum.tile([P, S], F32, name="warm", tag="bank7")
+        for i in range(3):
+            mx(warm[:], (x_q, picked_sc), 0, (x_q, picked_sc), slice(0, S), True, True)
+
         w1_grp = [sbuf("w1_grp%d" % t, [P, PACK], BF16) for t in range(PACK)]
         w1_cols = w1_raw[:].rearrange("p j (g t i) -> p t g i j", t=PACK, i=4)
 

@@ -111,11 +111,11 @@ def tile_picked_dmpnn8_relu_p_kernel(
         cast_w1(nc.scalar.copy, 3)
         cast_w1(nc.vector.tensor_copy, 0)
         cast_w1(nc.vector.tensor_copy, 1)
-        w1_mx = {t: quantize_w1(t) for t in (0, 1)}
+        w1_mx = {0: quantize_w1(0)}
         cast_w1(nc.vector.tensor_copy, 2)
-        w1_mx.update({3: quantize_w1(3)})
+        w1_mx.update({t: quantize_w1(t) for t in (1, 3)})
         for q in range(4):
-            y_piece(q, 0, q * QUARTER, QUARTER, w1_mx[0], (nc.vector.tensor_copy, nc.scalar.copy)[q % 2])
+            y_piece(q, 0, q * QUARTER, QUARTER, w1_mx[0], (nc.vector.tensor_copy, nc.scalar.copy)[q // 2])
         w1_mx.update({2: quantize_w1(2, "w1_0_codes")})
         for h in range(2):
             y_piece(4 + h, 1, h * HALF, HALF, w1_mx[1], nc.scalar.copy)

@@ -12,6 +12,7 @@ FP8X4 = mybir.dt.float8_e4m3fn_x4
 ADD = mybir.AluOpType.add
 SUB = mybir.AluOpType.subtract
 RELU = mybir.ActivationFunctionType.Relu
+COPY = mybir.ActivationFunctionType.Copy
 
 P = 128
 PACK = 4
@@ -19,7 +20,6 @@ K, T, S, N, H = 512, 2048, 512, 512, 512
 PER_COL = 16
 HALF = S // 2
 QUARTER = S // 4
-FIRST = HALF + QUARTER
 FLOPS = 2 * S * (K * N + K * H + H * N)
 
 
@@ -31,18 +31,22 @@ def tile_picked_dmpnn8_relu_p_kernel(
         keep = ctx.enter_context(tc.tile_pool(name="keep", bufs=1))
         psum = ctx.enter_context(tc.psum_pool(name="psum", bufs=1))
 
+        shared = ctx.enter_context(tc.tile_pool(name="shared", bufs=1))
+
         def sbuf(name, shape, dtype, tag=None):
             return keep.tile([P] + shape, dtype, name=name, tag=tag or name, align_bytes=64)
+
+        def placed(name, shape, dtype, offset):
+            return shared.tile([P] + shape, dtype, name=name, align_bytes=64, offset=offset)
 
         offs_sb = sbuf("offs_sb", [S // PER_COL], U16)
         in1_sb = sbuf("in1_sb", [S // PER_COL], U16)
         in2_sb = sbuf("in2_sb", [S // PER_COL], U16)
         rev_sb = sbuf("rev_sb", [S // PER_COL], U16)
-        words_all = sbuf("words_all", [T], I32)
+        words_all = placed("words_all", [T], I32, 0)
         scales_all = sbuf("scales_all", [T], U8)
         w1_raw = sbuf("w1_raw", [PACK, H], F32)
-        widths = (2 * S, 2 * S, 2 * FIRST, 2 * FIRST)
-        y = [sbuf("y%d" % t, [widths[t]], F32) for t in range(PACK)]
+        y = [sbuf("y%d" % t, [S], F32) for t in range(PACK)]
 
         nc.vector.memset(scales_all[:].bitcast(I32), 0)
         w1_rows = w1.rearrange("(p j) c -> p j c", j=PACK)
@@ -51,12 +55,10 @@ def tile_picked_dmpnn8_relu_p_kernel(
         nc.sync.dma_start(offs_sb[:], offs)
         nc.sync.dma_start(out=scales_all[0:P:8, :].bitcast(I32), in_=x_scales[0].bitcast(I32))
         nc.sync.dma_start(out=words_all[:, T // 2 : T], in_=x_rows[:, T // 2 : T])
-        nc.sync.dma_start(out=w1_raw[:], in_=w1_rows)
         nc.sync.dma_start(rev_sb[:], rev)
-        nc.sync.dma_start(in1_sb[:], in1)
         nc.sync.dma_start(in2_sb[:], in2)
-        for t in range(PACK):
-            nc.vector.memset(y[t][:, S : widths[t]], 0.0)
+        nc.sync.dma_start(out=w1_raw[:], in_=w1_rows)
+        nc.sync.dma_start(in1_sb[:], in1)
 
         x_sc = sbuf("x_sc", [S], U8)
         nc.vector.memset(x_sc[:].bitcast(I32), 0)
@@ -67,11 +69,12 @@ def tile_picked_dmpnn8_relu_p_kernel(
             nc.sync.dma_start(out=x_sc[r:P:32, :].bitcast(I32), in_=picked_sc[8 * r : P : 32, :].bitcast(I32))
         nc.vector.tensor_copy(x_q[:], words_all[:].bitcast(U32).indirect(offs_sb[:]))
         x_mx = (x_q, x_sc)
-        w23_raw = sbuf("w23_raw", [2, PACK, N], F32, "scales_all")
-        nc.sync.dma_start(out=w23_raw[:, 0], in_=w2.rearrange("(p j) c -> p j c", j=PACK))
+        w2_raw = sbuf("w2_raw", [PACK, N], F32, "scales_all")
+        w3_raw = placed("w3_raw", [PACK, N], F32, 0)
+        nc.sync.dma_start(out=w2_raw[:], in_=w2.rearrange("(p j) c -> p j c", j=PACK))
         w3_rows = w3.rearrange("(g t i) c -> i g t c", t=PACK, i=4)
         for i in range(4):
-            nc.sync.dma_start(out=w23_raw[i:P:4, 1], in_=w3_rows[i])
+            nc.sync.dma_start(out=w3_raw[i:P:4], in_=w3_rows[i])
 
         def quantize(name, grouped, width, tag=None):
             codes = sbuf(name + "_codes", [width], U32, tag)
@@ -89,10 +92,6 @@ def tile_picked_dmpnn8_relu_p_kernel(
                 start=start,
                 stop=stop,
             )
-
-        warm = psum.tile([P, S], F32, name="warm", tag="bank7")
-        for i in range(3):
-            mx(warm[:], (x_q, picked_sc), 0, (x_q, picked_sc), slice(0, S), True, True)
 
         w1_grp = [sbuf("w1_grp%d" % t, [P, PACK], BF16) for t in range(PACK)]
         w1_cols = w1_raw[:].rearrange("p j (g t i) -> p t g i j", t=PACK, i=4)
@@ -117,61 +116,48 @@ def tile_picked_dmpnn8_relu_p_kernel(
         for q in range(4):
             y_piece(q, 0, q * QUARTER, QUARTER, w1_mx[0], (nc.vector.tensor_copy, nc.scalar.copy)[q // 2])
         w1_mx.update({2: quantize_w1(2, "w1_0_codes")})
-        for h in range(2):
-            y_piece(4 + h, 1, h * HALF, HALF, w1_mx[1], nc.scalar.copy)
-        y_piece(6, 2, 0, S, w1_mx[2], nc.scalar.copy)
-        y_piece(5, 3, 0, S, w1_mx[3], nc.scalar.copy)
-
-        def weave(copy, dst, src):
-            copy(dst.rearrange("p (c i) t -> p c t i", i=4), src.rearrange("p t (c i) -> p c t i", i=4))
-
-        def weight(name, raw):
-            grp = sbuf(name + "_grp", [N, PACK], BF16)
-            weave(nc.scalar.copy, grp[:], raw)
-            return grp[:].rearrange("p c j -> p (c j)")
-
-        w2_grp = weight("w2", w23_raw[:, 0])
-        w3_grp = weight("w3", w23_raw[:, 1])
 
         def entries(tile, c0, n):
             return tile[:, c0 // PER_COL : (c0 + n) // PER_COL]
 
-        narrow = [sbuf("narrow%d" % v, [S], F32) for v in range(2)]
-        for v in range(2):
-            nc.scalar.copy(narrow[v][:], y[2 + v][:, 0:S])
+        spans = ((0, HALF), (HALF, QUARTER), (HALF + QUARTER, QUARTER))
+        part = [sbuf("part%d" % h, [PACK, HALF], F32) for h in range(2)]
 
-        def gather_run(name, windows, c0, n, back, part):
-            z = sbuf("z" + name, [2, n], F32)
-            for v in range(2):
-                nc.vector.tensor_copy(back[v], windows[v][:].indirect(entries(rev_sb, c0, n)))
-            for v in range(2):
-                nc.vector.tensor_tensor(part[v], windows[v][:].indirect(entries(in1_sb, c0, n)), back[v], SUB)
-            for v in range(2):
-                nc.vector.tensor_tensor(z[:, v, :], windows[v][:].indirect(entries(in2_sb, c0, n)), part[v], ADD)
-            return z
+        back = {}
 
-        def rows(name, count, n, tag=None):
-            tile = sbuf(name, [count, n], F32, tag)
-            return [tile[:, v, :] for v in range(count)]
+        def fetch_rev(h, t):
+            back[h, t] = placed("back%d_%d" % (h, t), [HALF], F32, 4 * HALF * (PACK * h + t))
+            nc.scalar.activation(back[h, t][:], y[t][:].indirect(entries(rev_sb, h * HALF, HALF)), COPY)
 
-        spans = ((0, HALF), (HALF, QUARTER), (FIRST, QUARTER))
-        z_low = gather_run("_low", y[0:2], 0, S, rows("first_low", 1, S) + rows("second_low", 1, S), rows("part_low", 2, S, "w1_3_codes"))
-        high = rows("first_high", 1, FIRST, "first_low") + rows("rest_high", 3, FIRST)
-        z_high = gather_run("_high", y[2:4], 0, FIRST, high[0:2], high[2:4])
-        w2_mx = quantize("w2", w2_grp, N, "first_low")
-        w3_mx = quantize("w3", w3_grp, N)
-        z_grp = sbuf("z_grp", [S, PACK], BF16, "scales_all")
-        weave(nc.scalar.copy, z_grp[:, :, 0:2], z_low[:])
+        def fetch_in2(i, t):
+            nc.scalar.activation(other[i][:, t, :], y[t][:].indirect(entries(in2_sb, *spans[i])), COPY)
 
-        def quantize_z(i, copy, planes):
+        def fetch_in1(c0, n, t):
+            h, at = divmod(c0, HALF)
+            nc.vector.tensor_tensor(part[h][:, t, at : at + n], y[t][:].indirect(entries(in1_sb, c0, n)), back[h, t][:, at : at + n], SUB)
+
+        def weight(name, raw):
+            grp = [sbuf("%s_grp%d" % (name, h), [HALF, PACK], BF16) for h in range(2)]
+            for h in range(2):
+                nc.vector.tensor_copy(grp[h][:], raw[:, :, h * HALF : (h + 1) * HALF].rearrange("p j c -> p c j"))
+            codes = sbuf(name + "_codes", [N], U32)
+            scales = sbuf(name + "_scales", [N], U8)
+            for h in range(2):
+                cols = slice(h * HALF, (h + 1) * HALF)
+                nc.vector.quantize_mx(out=codes[:, cols].bitcast(FP8X4), scales=scales[:, cols], in_=grp[h][:].rearrange("p c j -> p (c j)"))
+            return codes, scales
+
+        def sum_z(i):
             c0, n = spans[i]
-            weave(copy, z_grp[:, c0 : c0 + n, 2:4], planes)
-            return quantize("z%d" % i, z_grp[:, c0 : c0 + n, :].rearrange("p c t -> p (c t)"), n)
-
-        z_mx = [quantize_z(0, nc.scalar.copy, z_high[:, :, 0:HALF]), quantize_z(1, nc.scalar.copy, z_high[:, :, HALF:FIRST])]
-        last = rows("first_last", 1, QUARTER, "z_low") + rows("rest_last", 3, QUARTER, "z_high")
-        z_last = gather_run("_last", narrow, FIRST, QUARTER, last[0:2], last[2:4])
-        z_mx.append(quantize_z(2, nc.vector.tensor_copy, z_last[:]))
+            h, at = divmod(c0, HALF)
+            grp = sbuf("z%d_grp" % i, [n, PACK], BF16)
+            nc.vector.tensor_tensor(
+                grp[:].rearrange("p (c i) t -> p c t i", i=2),
+                part[h][:, :, at : at + n].rearrange("p t (c i) -> p c t i", i=2),
+                other[i].rearrange("p t (c i) -> p c t i", i=2),
+                ADD,
+            )
+            return grp[:].rearrange("p c t -> p (c t)")
 
         out_rows = out.rearrange("(u p) j -> p u j", p=P)
 
@@ -181,34 +167,58 @@ def tile_picked_dmpnn8_relu_p_kernel(
         def relu_vector(dst, src):
             nc.vector.tensor_scalar_max(dst, src, 0.0)
 
-        def products(name, parts, relus, tags, ahead, stores):
-            base = spans[parts[0]][0]
-            width = sum(spans[i][1] for i in parts)
-            banks = [psum.tile([P, width], F32, name="%s_bank%d" % (name, u), tag="bank%d" % tags[u]) for u in range(PACK)]
-            res = sbuf(name, [PACK, width], F32)
-
-            def h0_passes(u, start, stop):
-                for i in parts:
-                    c0, n = spans[i]
-                    dst = banks[u][:, c0 - base : c0 - base + n]
-                    mx(dst, w2_mx, u, x_mx, slice(c0, c0 + n), start and i == parts[0], stop and i == parts[-1])
-
-            def z_passes(u, start, stop):
-                for i in parts:
-                    c0, n = spans[i]
-                    dst = banks[u][:, c0 - base : c0 - base + n]
-                    mx(dst, w3_mx, u, z_mx[i], slice(0, n), start and i == parts[0], stop and i == parts[-1])
-
-            for u in range(ahead):
-                h0_passes(u, True, False)
+        def open_banks(i, tags):
+            c0, n = spans[i]
+            banks = [psum.tile([P, n], F32, name="o%d_bank%d" % (i, u), tag="bank%d" % tags[u]) for u in range(PACK)]
             for u in range(PACK):
-                z_passes(u, u >= ahead, u < ahead)
-                if u >= ahead:
-                    h0_passes(u, False, True)
+                mx(banks[u][:], w2_mx, u, x_mx, slice(c0, c0 + n), True, False)
+            return banks
+
+        def finish(i, banks, z_mx, relus, stores):
+            c0, n = spans[i]
+            res = sbuf("res%d" % i, [PACK, n], F32)
+            for u in range(PACK):
+                mx(banks[u][:], w3_mx, u, z_mx, slice(0, n), False, True)
                 relus[u](res[:, u, :], banks[u][:])
                 if u in stores:
                     rows_out = slice(stores[u], u + 1)
-                    nc.sync.dma_start(out=out_rows[:, rows_out, base : base + width], in_=res[:, rows_out, :])
+                    nc.sync.dma_start(out=out_rows[:, rows_out, c0 : c0 + n], in_=res[:, rows_out, :])
 
-        products("res_first", (0, 1), (relu_scalar,) * 4, (0, 1, 2, 3), 2, {0: 0, 1: 1, 2: 2, 3: 3})
-        products("res_last", (2,), (relu_scalar, relu_vector) * 2, (0, 1, 4, 5), 4, {0: 0, 1: 1, 3: 2})
+        other_first = sbuf("other_first", [PACK, HALF], F32)
+        other = [other_first[:]]
+        y_piece(4, 1, 0, HALF, w1_mx[1], nc.vector.tensor_copy)
+        fetch_in2(0, 0)
+        y_piece(7, 1, HALF, HALF, w1_mx[1], nc.scalar.copy)
+        for t in (2, 3):
+            y_piece(3 + t, t, 0, S, w1_mx[t], nc.scalar.copy)
+        for t in (1, 2, 3):
+            fetch_in2(0, t)
+        w2_mx = weight("w2", w2_raw)
+        w3_mx = weight("w3", w3_raw)
+        for i in (1, 2):
+            other.append(sbuf("other%d" % i, [PACK, QUARTER], F32, "w3_grp%d" % (i - 1))[:])
+        for h in range(2):
+            for t in range(PACK):
+                fetch_rev(h, t)
+        for t in range(PACK):
+            fetch_in1(0, HALF, t)
+        banks0 = open_banks(0, (0, 1, 2, 3))
+        banks1 = open_banks(1, (4, 5, 6, 7))
+        for i in (1, 2):
+            for t in range(PACK):
+                fetch_in2(i, t)
+        fetch_in1(HALF, HALF, 0)
+        z0_grp = sum_z(0)
+        fetch_in1(HALF, HALF, 1)
+        z0_mx = quantize("z0", z0_grp, spans[0][1])
+        finish(0, banks0, z0_mx, (relu_scalar,) * 4, {1: 0, 3: 2})
+        banks2 = open_banks(2, (0, 1, 2, 3))
+        fetch_in1(HALF, HALF, 2)
+        fetch_in1(*spans[1], 3)
+        fetch_in1(*spans[2], 3)
+        z1_grp = sum_z(1)
+        z2_grp = sum_z(2)
+        z1_mx = quantize("z1", z1_grp, spans[1][1])
+        z2_mx = quantize("z2", z2_grp, spans[2][1])
+        finish(1, banks1, z1_mx, (relu_scalar,) * 4, {1: 0, 3: 2})
+        finish(2, banks2, z2_mx, (relu_scalar, relu_vector) * 2, {0: 0, 1: 1, 3: 2})

@@ -20,6 +20,7 @@ K, T, S, N, H = 512, 2048, 512, 512, 512
 PER_COL = 16
 HALF = S // 2
 QUARTER = S // 4
+KIB = 1024
 FLOPS = 2 * S * (K * N + K * H + H * N)
 
 
@@ -43,8 +44,8 @@ def tile_picked_dmpnn8_relu_p_kernel(
         in1_sb = sbuf("in1_sb", [S // PER_COL], U16)
         in2_sb = sbuf("in2_sb", [S // PER_COL], U16)
         rev_sb = sbuf("rev_sb", [S // PER_COL], U16)
-        words_all = placed("words_all", [T], I32, 0)
-        scales_all = sbuf("scales_all", [T], U8)
+        words_all = placed("words_all", [T], I32, 1 * KIB)
+        scales_all = placed("scales_all", [T], U8, 13 * KIB)
         w1_raw = sbuf("w1_raw", [PACK, H], F32)
         y = [sbuf("y%d" % t, [S], F32) for t in range(PACK)]
 
@@ -69,8 +70,8 @@ def tile_picked_dmpnn8_relu_p_kernel(
             nc.sync.dma_start(out=x_sc[r:P:32, :].bitcast(I32), in_=picked_sc[8 * r : P : 32, :].bitcast(I32))
         nc.vector.tensor_copy(x_q[:], words_all[:].bitcast(U32).indirect(offs_sb[:]))
         x_mx = (x_q, x_sc)
-        w2_raw = sbuf("w2_raw", [PACK, N], F32, "scales_all")
-        w3_raw = placed("w3_raw", [PACK, N], F32, 0)
+        w2_raw = placed("w2_raw", [PACK, N], F32, 13 * KIB)
+        w3_raw = placed("w3_raw", [PACK, N], F32, 1 * KIB)
         nc.sync.dma_start(out=w2_raw[:], in_=w2.rearrange("(p j) c -> p j c", j=PACK))
         w3_rows = w3.rearrange("(g t i) c -> i g t c", t=PACK, i=4)
         for i in range(4):
@@ -121,40 +122,44 @@ def tile_picked_dmpnn8_relu_p_kernel(
             return tile[:, c0 // PER_COL : (c0 + n) // PER_COL]
 
         spans = ((0, HALF), (HALF, QUARTER), (HALF + QUARTER, QUARTER))
-        part = [sbuf("part%d" % h, [PACK, HALF], F32) for h in range(2)]
+        part = {1: sbuf("part1", [PACK, HALF], F32)}
 
         back = {}
 
         def fetch_rev(h, t):
-            back[h, t] = placed("back%d_%d" % (h, t), [HALF], F32, 4 * HALF * (PACK * h + t))
+            name = "back%d_%d" % (h, t)
+            back[h, t] = placed(name, [HALF], F32, ((13, 2)[h] + t) * KIB) if h or t else sbuf(name, [HALF], F32)
             nc.scalar.activation(back[h, t][:], y[t][:].indirect(entries(rev_sb, h * HALF, HALF)), COPY)
 
-        def fetch_in2(i, t):
-            nc.scalar.activation(other[i][:, t, :], y[t][:].indirect(entries(in2_sb, *spans[i])), COPY)
+        def fetch_in2(h, t):
+            nc.scalar.activation(other[h][:, t, :], y[t][:].indirect(entries(in2_sb, h * HALF, HALF)), COPY)
 
         def fetch_in1(c0, n, t):
             h, at = divmod(c0, HALF)
             nc.vector.tensor_tensor(part[h][:, t, at : at + n], y[t][:].indirect(entries(in1_sb, c0, n)), back[h, t][:, at : at + n], SUB)
 
-        def weight(name, raw):
+        def weight(name, raw, between):
             grp = [sbuf("%s_grp%d" % (name, h), [HALF, PACK], BF16) for h in range(2)]
             for h in range(2):
                 nc.vector.tensor_copy(grp[h][:], raw[:, :, h * HALF : (h + 1) * HALF].rearrange("p j c -> p c j"))
             codes = sbuf(name + "_codes", [N], U32)
             scales = sbuf(name + "_scales", [N], U8)
             for h in range(2):
+                if h:
+                    between()
                 cols = slice(h * HALF, (h + 1) * HALF)
                 nc.vector.quantize_mx(out=codes[:, cols].bitcast(FP8X4), scales=scales[:, cols], in_=grp[h][:].rearrange("p c j -> p (c j)"))
             return codes, scales
 
-        def sum_z(i):
+        def sum_z(i, offset=None):
             c0, n = spans[i]
             h, at = divmod(c0, HALF)
-            grp = sbuf("z%d_grp" % i, [n, PACK], BF16)
+            name = "z%d_grp" % i
+            grp = sbuf(name, [n, PACK], BF16) if offset is None else placed(name, [n, PACK], BF16, offset)
             nc.vector.tensor_tensor(
                 grp[:].rearrange("p (c i) t -> p c t i", i=2),
                 part[h][:, :, at : at + n].rearrange("p t (c i) -> p c t i", i=2),
-                other[i].rearrange("p t (c i) -> p c t i", i=2),
+                other[h][:, :, at : at + n].rearrange("p t (c i) -> p c t i", i=2),
                 ADD,
             )
             return grp[:].rearrange("p c t -> p (c t)")
@@ -184,38 +189,42 @@ def tile_picked_dmpnn8_relu_p_kernel(
                     rows_out = slice(stores[u], u + 1)
                     nc.sync.dma_start(out=out_rows[:, rows_out, c0 : c0 + n], in_=res[:, rows_out, :])
 
-        other_first = sbuf("other_first", [PACK, HALF], F32)
-        other = [other_first[:]]
-        y_piece(4, 1, 0, HALF, w1_mx[1], nc.vector.tensor_copy)
-        fetch_in2(0, 0)
-        y_piece(7, 1, HALF, HALF, w1_mx[1], nc.scalar.copy)
-        for t in (2, 3):
-            y_piece(3 + t, t, 0, S, w1_mx[t], nc.scalar.copy)
+        other = {}
+        y_piece(4, 1, 0, S, w1_mx[1], nc.vector.tensor_copy)
+        fetch_rev(0, 0)
+        y_piece(5, 2, 0, S, w1_mx[2], nc.scalar.copy)
+        y_piece(6, 3, 0, S, w1_mx[3], nc.scalar.copy)
+
+        def first_in1():
+            part[0] = placed("part0", [PACK, HALF], F32, 17 * KIB)
+            fetch_in1(0, HALF, 0)
+
+        w2_mx = weight("w2", w2_raw, first_in1)
+        other[0] = placed("other0", [PACK, HALF], F32, 10 * KIB)
         for t in (1, 2, 3):
-            fetch_in2(0, t)
-        w2_mx = weight("w2", w2_raw)
-        w3_mx = weight("w3", w3_raw)
-        for i in (1, 2):
-            other.append(sbuf("other%d" % i, [PACK, QUARTER], F32, "w3_grp%d" % (i - 1))[:])
-        for h in range(2):
-            for t in range(PACK):
-                fetch_rev(h, t)
+            fetch_rev(0, t)
         for t in range(PACK):
+            fetch_in2(0, t)
+        for t in (1, 2, 3):
             fetch_in1(0, HALF, t)
+        w3_mx = weight("w3", w3_raw, lambda: None)
+        for t in range(PACK):
+            fetch_rev(1, t)
         banks0 = open_banks(0, (0, 1, 2, 3))
         banks1 = open_banks(1, (4, 5, 6, 7))
-        for i in (1, 2):
-            for t in range(PACK):
-                fetch_in2(i, t)
+        other[1] = placed("other1", [PACK, HALF], F32, 6 * KIB)
+        for t in (0, 1, 2):
+            fetch_in2(1, t)
+        z0_grp = sum_z(0, 0)
         fetch_in1(HALF, HALF, 0)
-        z0_grp = sum_z(0)
-        fetch_in1(HALF, HALF, 1)
         z0_mx = quantize("z0", z0_grp, spans[0][1])
         finish(0, banks0, z0_mx, (relu_scalar,) * 4, {1: 0, 3: 2})
         banks2 = open_banks(2, (0, 1, 2, 3))
+        fetch_in1(HALF, HALF, 1)
         fetch_in1(HALF, HALF, 2)
-        fetch_in1(*spans[1], 3)
-        fetch_in1(*spans[2], 3)
+        fetch_in1(HALF, HALF, 3)
+        nc.vector.tensor_copy(other[1][:, 3, 0:QUARTER], y[3][:].indirect(entries(in2_sb, *spans[1])))
+        nc.vector.tensor_copy(other[1][:, 3, QUARTER:HALF], y[3][:].indirect(entries(in2_sb, *spans[2])))
         z1_grp = sum_z(1)
         z2_grp = sum_z(2)
         z1_mx = quantize("z1", z1_grp, spans[1][1])

@@ -141,7 +141,10 @@ def tile_picked_dmpnn8_relu_p_kernel(
         def weight(name, raw, between):
             grp = [sbuf("%s_grp%d" % (name, h), [HALF, PACK], BF16) for h in range(2)]
             for h in range(2):
-                nc.vector.tensor_copy(grp[h][:], raw[:, :, h * HALF : (h + 1) * HALF].rearrange("p j c -> p c j"))
+                nc.vector.tensor_copy(
+                    grp[h][:].rearrange("p (c i) j -> p c j i", i=4),
+                    raw[:, :, h * HALF : (h + 1) * HALF].rearrange("p j (c i) -> p c j i", i=4),
+                )
             codes = sbuf(name + "_codes", [N], U32)
             scales = sbuf(name + "_scales", [N], U8)
             for h in range(2):

@@ -95,10 +95,10 @@ def tile_picked_dmpnn8_relu_p_kernel(
             )
 
         w1_grp = [sbuf("w1_grp%d" % t, [P, PACK], BF16) for t in range(PACK)]
-        w1_cols = w1_raw[:].rearrange("p j (g t i) -> p t g i j", t=PACK, i=4)
+        w1_cols = w1_raw[:].rearrange("p j (g t i) -> p t g j i", t=PACK, i=4)
 
         def cast_w1(copy, t):
-            copy(w1_grp[t][:].rearrange("p (g i) j -> p g i j", i=4), w1_cols[:, t])
+            copy(w1_grp[t][:].rearrange("p (g i) j -> p g j i", i=4), w1_cols[:, t])
 
         def quantize_w1(t, tag=None):
             return quantize("w1_%d" % t, w1_grp[t][:].rearrange("p m j -> p (m j)"), P, tag)
@@ -160,9 +160,9 @@ def tile_picked_dmpnn8_relu_p_kernel(
             name = "z%d_grp" % i
             grp = sbuf(name, [n, PACK], BF16) if offset is None else placed(name, [n, PACK], BF16, offset)
             nc.vector.tensor_tensor(
-                grp[:].rearrange("p (c i) t -> p c t i", i=2),
-                part[h][:, :, at : at + n].rearrange("p t (c i) -> p c t i", i=2),
-                other[h][:, :, at : at + n].rearrange("p t (c i) -> p c t i", i=2),
+                grp[:].rearrange("p (c i) t -> p c t i", i=4),
+                part[h][:, :, at : at + n].rearrange("p t (c i) -> p c t i", i=4),
+                other[h][:, :, at : at + n].rearrange("p t (c i) -> p c t i", i=4),
                 ADD,
             )
             return grp[:].rearrange("p c t -> p (c t)")

@@ -57,8 +57,8 @@ def tile_picked_dmpnn8_relu_p_kernel(
         nc.sync.dma_start(out=scales_all[0:P:8, :].bitcast(I32), in_=x_scales[0].bitcast(I32))
         nc.sync.dma_start(out=words_all[:, T // 2 : T], in_=x_rows[:, T // 2 : T])
         nc.sync.dma_start(rev_sb[:], rev)
-        nc.sync.dma_start(in2_sb[:], in2)
         nc.sync.dma_start(out=w1_raw[:], in_=w1_rows)
+        nc.sync.dma_start(in2_sb[:], in2)
         nc.sync.dma_start(in1_sb[:], in1)
 
         x_sc = sbuf("x_sc", [S], U8)
@@ -122,13 +122,12 @@ def tile_picked_dmpnn8_relu_p_kernel(
             return tile[:, c0 // PER_COL : (c0 + n) // PER_COL]
 
         spans = ((0, HALF), (HALF, QUARTER), (HALF + QUARTER, QUARTER))
-        part = {1: sbuf("part1", [PACK, HALF], F32)}
+        part = {}
 
         back = {}
 
         def fetch_rev(h, t):
-            name = "back%d_%d" % (h, t)
-            back[h, t] = placed(name, [HALF], F32, ((13, 2)[h] + t) * KIB) if h or t else sbuf(name, [HALF], F32)
+            back[h, t] = sbuf("back%d_%d" % (h, t), [HALF], F32)
             nc.scalar.activation(back[h, t][:], y[t][:].indirect(entries(rev_sb, h * HALF, HALF)), COPY)
 
         def fetch_in2(h, t):
@@ -175,18 +174,26 @@ def tile_picked_dmpnn8_relu_p_kernel(
         def relu_vector(dst, src):
             nc.vector.tensor_scalar_max(dst, src, 0.0)
 
-        def open_banks(i, tags):
+        def take_banks(i, first):
+            return [psum.tile([P, spans[i][1]], F32, name="o%d_bank%d" % (i, u), tag="bank%d" % (first + u)) for u in range(PACK)]
+
+        def h0_pass(i, bank, u, opens):
             c0, n = spans[i]
-            banks = [psum.tile([P, n], F32, name="o%d_bank%d" % (i, u), tag="bank%d" % tags[u]) for u in range(PACK)]
+            mx(bank[:], w2_mx, u, x_mx, slice(c0, c0 + n), opens, not opens)
+
+        def open_banks(i, first):
+            banks = take_banks(i, first)
             for u in range(PACK):
-                mx(banks[u][:], w2_mx, u, x_mx, slice(c0, c0 + n), True, False)
+                h0_pass(i, banks[u], u, True)
             return banks
 
-        def finish(i, banks, z_mx, relus, stores):
+        def finish(i, banks, opened, z_mx, relus, stores):
             c0, n = spans[i]
             res = sbuf("res%d" % i, [PACK, n], F32)
             for u in range(PACK):
-                mx(banks[u][:], w3_mx, u, z_mx, slice(0, n), False, True)
+                mx(banks[u][:], w3_mx, u, z_mx, slice(0, n), not opened, opened)
+                if not opened:
+                    h0_pass(i, banks[u], u, False)
                 relus[u](res[:, u, :], banks[u][:])
                 if u in stores:
                     rows_out = slice(stores[u], u + 1)
@@ -203,7 +210,7 @@ def tile_picked_dmpnn8_relu_p_kernel(
             fetch_in1(0, HALF, 0)
 
         w2_mx = weight("w2", w2_raw, first_in1)
-        other[0] = placed("other0", [PACK, HALF], F32, 10 * KIB)
+        other[0] = sbuf("other0", [PACK, HALF], F32)
         for t in (1, 2, 3):
             fetch_rev(0, t)
         for t in range(PACK):
@@ -213,24 +220,26 @@ def tile_picked_dmpnn8_relu_p_kernel(
         w3_mx = weight("w3", w3_raw, lambda: None)
         for t in range(PACK):
             fetch_rev(1, t)
-        banks0 = open_banks(0, (0, 1, 2, 3))
-        banks1 = open_banks(1, (4, 5, 6, 7))
+        banks2 = open_banks(2, 4)
         other[1] = placed("other1", [PACK, HALF], F32, 6 * KIB)
+        part[1] = placed("part1", [PACK, HALF], F32, 2 * KIB)
         for t in (0, 1, 2):
             fetch_in2(1, t)
+        nc.scalar.activation(other[1][:, 3, QUARTER:HALF], y[3][:].indirect(entries(in2_sb, *spans[2])), COPY)
         z0_grp = sum_z(0, 0)
         fetch_in1(HALF, HALF, 0)
         z0_mx = quantize("z0", z0_grp, spans[0][1])
-        finish(0, banks0, z0_mx, (relu_scalar,) * 4, {1: 0, 3: 2})
-        banks2 = open_banks(2, (0, 1, 2, 3))
+        finish(0, take_banks(0, 0), False, z0_mx, (relu_scalar,) * 4, {1: 0, 3: 2})
+        banks1 = open_banks(1, 0)
         fetch_in1(HALF, HALF, 1)
-        fetch_in1(HALF, HALF, 2)
-        fetch_in1(HALF, HALF, 3)
+        fetch_in1(*spans[1], 2)
         nc.vector.tensor_copy(other[1][:, 3, 0:QUARTER], y[3][:].indirect(entries(in2_sb, *spans[1])))
-        nc.vector.tensor_copy(other[1][:, 3, QUARTER:HALF], y[3][:].indirect(entries(in2_sb, *spans[2])))
+        fetch_in1(*spans[1], 3)
+        fetch_in1(*spans[2], 2)
         z1_grp = sum_z(1)
-        z2_grp = sum_z(2)
+        fetch_in1(*spans[2], 3)
         z1_mx = quantize("z1", z1_grp, spans[1][1])
+        z2_grp = sum_z(2)
+        finish(1, banks1, True, z1_mx, (relu_vector,) + (relu_scalar,) * 3, {1: 0, 3: 2})
         z2_mx = quantize("z2", z2_grp, spans[2][1])
-        finish(1, banks1, z1_mx, (relu_scalar,) * 4, {1: 0, 3: 2})
-        finish(2, banks2, z2_mx, (relu_scalar, relu_vector) * 2, {0: 0, 1: 1, 3: 2})
+        finish(2, banks2, True, z2_mx, (relu_scalar, relu_vector) * 2, {0: 0, 1: 1, 3: 2})

@@ -200,7 +200,8 @@ def tile_picked_dmpnn8_relu_p_kernel(
                     nc.sync.dma_start(out=out_rows[:, rows_out, c0 : c0 + n], in_=res[:, rows_out, :])
 
         other = {}
-        y_piece(4, 1, 0, S, w1_mx[1], nc.vector.tensor_copy)
+        y_piece(4, 1, 0, HALF, w1_mx[1], nc.vector.tensor_copy)
+        y_piece(7, 1, HALF, HALF, w1_mx[1], nc.vector.tensor_copy)
         fetch_rev(0, 0)
         y_piece(5, 2, 0, S, w1_mx[2], nc.scalar.copy)
         y_piece(6, 3, 0, S, w1_mx[3], nc.scalar.copy)

@@ -181,9 +181,9 @@ def tile_picked_dmpnn8_relu_p_kernel(
             c0, n = spans[i]
             mx(bank[:], w2_mx, u, x_mx, slice(c0, c0 + n), opens, not opens)
 
-        def open_banks(i, first):
+        def open_banks(i, first, count):
             banks = take_banks(i, first)
-            for u in range(PACK):
+            for u in range(count):
                 h0_pass(i, banks[u], u, True)
             return banks
 
@@ -191,8 +191,8 @@ def tile_picked_dmpnn8_relu_p_kernel(
             c0, n = spans[i]
             res = sbuf("res%d" % i, [PACK, n], F32)
             for u in range(PACK):
-                mx(banks[u][:], w3_mx, u, z_mx, slice(0, n), not opened, opened)
-                if not opened:
+                mx(banks[u][:], w3_mx, u, z_mx, slice(0, n), u >= opened, u < opened)
+                if u >= opened:
                     h0_pass(i, banks[u], u, False)
                 relus[u](res[:, u, :], banks[u][:])
                 if u in stores:
@@ -221,7 +221,7 @@ def tile_picked_dmpnn8_relu_p_kernel(
         w3_mx = weight("w3", w3_raw, lambda: None)
         for t in range(PACK):
             fetch_rev(1, t)
-        banks2 = open_banks(2, 4)
+        banks1 = open_banks(1, 4, PACK)
         other[1] = placed("other1", [PACK, HALF], F32, 6 * KIB)
         part[1] = placed("part1", [PACK, HALF], F32, 2 * KIB)
         for t in (0, 1, 2):
@@ -230,8 +230,8 @@ def tile_picked_dmpnn8_relu_p_kernel(
         z0_grp = sum_z(0, 0)
         fetch_in1(HALF, HALF, 0)
         z0_mx = quantize("z0", z0_grp, spans[0][1])
-        finish(0, take_banks(0, 0), False, z0_mx, (relu_scalar,) * 4, {1: 0, 3: 2})
-        banks1 = open_banks(1, 0)
+        finish(0, take_banks(0, 0), 0, z0_mx, (relu_scalar,) * 4, {1: 0, 3: 2})
+        banks2 = open_banks(2, 0, PACK - 1)
         fetch_in1(HALF, HALF, 1)
         fetch_in1(*spans[1], 2)
         nc.vector.tensor_copy(other[1][:, 3, 0:QUARTER], y[3][:].indirect(entries(in2_sb, *spans[1])))
@@ -241,6 +241,6 @@ def tile_picked_dmpnn8_relu_p_kernel(
         fetch_in1(*spans[2], 3)
         z1_mx = quantize("z1", z1_grp, spans[1][1])
         z2_grp = sum_z(2)
-        finish(1, banks1, True, z1_mx, (relu_vector,) + (relu_scalar,) * 3, {1: 0, 3: 2})
+        finish(1, banks1, PACK, z1_mx, (relu_vector, relu_scalar) * 2, {1: 0, 3: 2})
         z2_mx = quantize("z2", z2_grp, spans[2][1])
-        finish(2, banks2, True, z2_mx, (relu_scalar, relu_vector) * 2, {0: 0, 1: 1, 3: 2})
+        finish(2, banks2, PACK - 1, z2_mx, (relu_scalar, relu_vector) * 2, {0: 0, 1: 1, 3: 2})

@@ -21,6 +21,7 @@ PER_COL = 16
 HALF = S // 2
 QUARTER = S // 4
 KIB = 1024
+APART = 32 * KIB
 FLOPS = 2 * S * (K * N + K * H + H * N)
 
 
@@ -35,10 +36,10 @@ def tile_picked_dmpnn8_relu_p_kernel(
         shared = ctx.enter_context(tc.tile_pool(name="shared", bufs=1))
 
         def sbuf(name, shape, dtype, tag=None):
-            return keep.tile([P] + shape, dtype, name=name, tag=tag or name, align_bytes=64)
+            return keep.tile([P] + shape, dtype, name=name, tag=tag or name, align_bytes=256)
 
         def placed(name, shape, dtype, offset):
-            return shared.tile([P] + shape, dtype, name=name, align_bytes=64, offset=offset)
+            return shared.tile([P] + shape, dtype, name=name, align_bytes=256, offset=offset)
 
         offs_sb = sbuf("offs_sb", [S // PER_COL], U16)
         in1_sb = sbuf("in1_sb", [S // PER_COL], U16)
@@ -47,7 +48,7 @@ def tile_picked_dmpnn8_relu_p_kernel(
         words_all = placed("words_all", [T], I32, 1 * KIB)
         scales_all = placed("scales_all", [T], U8, 13 * KIB)
         w1_raw = sbuf("w1_raw", [PACK, H], F32)
-        y = [sbuf("y%d" % t, [S], F32) for t in range(PACK)]
+        y = [placed("y%d" % t, [S], F32, (t + 1) * APART) for t in range(PACK)]
 
         nc.vector.memset(scales_all[:].bitcast(I32), 0)
         w1_rows = w1.rearrange("(p j) c -> p j c", j=PACK)
@@ -127,7 +128,7 @@ def tile_picked_dmpnn8_relu_p_kernel(
         back = {}
 
         def fetch_rev(h, t):
-            back[h, t] = sbuf("back%d_%d" % (h, t), [HALF], F32)
+            back[h, t] = placed("back%d_%d" % (h, t), [HALF], F32, 5 * APART + (h * PACK + t) * KIB)
             nc.scalar.activation(back[h, t][:], y[t][:].indirect(entries(rev_sb, h * HALF, HALF)), COPY)
 
         def fetch_in2(h, t):

@@ -228,6 +228,7 @@ def tile_picked_dmpnn8_relu_p_kernel(
         for t in (0, 1, 2):
             fetch_in2(1, t)
         nc.scalar.activation(other[1][:, 3, QUARTER:HALF], y[3][:].indirect(entries(in2_sb, *spans[2])), COPY)
+        nc.vector.tensor_copy(other[1][:, 3, 0:QUARTER], y[3][:].indirect(entries(in2_sb, *spans[1])))
         z0_grp = sum_z(0, 0)
         fetch_in1(HALF, HALF, 0)
         z0_mx = quantize("z0", z0_grp, spans[0][1])
@@ -235,7 +236,6 @@ def tile_picked_dmpnn8_relu_p_kernel(
         banks2 = open_banks(2, 0, PACK - 1)
         fetch_in1(HALF, HALF, 1)
         fetch_in1(*spans[1], 2)
-        nc.vector.tensor_copy(other[1][:, 3, 0:QUARTER], y[3][:].indirect(entries(in2_sb, *spans[1])))
         fetch_in1(*spans[1], 3)
         fetch_in1(*spans[2], 2)
         z1_grp = sum_z(1)

from contextlib import ExitStack

import concourse.mybir as mybir

F32 = mybir.dt.float32
BF16 = mybir.dt.bfloat16
I32 = mybir.dt.int32
U32 = mybir.dt.uint32
U16 = mybir.dt.uint16
U8 = mybir.dt.uint8
FP8X4 = mybir.dt.float8_e4m3fn_x4
ADD = mybir.AluOpType.add
SUB = mybir.AluOpType.subtract
RELU = mybir.ActivationFunctionType.Relu
COPY = mybir.ActivationFunctionType.Copy

P = 128
PACK = 4
K, T, S, N, H = 512, 2048, 512, 512, 512
PER_COL = 16
HALF = S // 2
QUARTER = S // 4
KIB = 1024
APART = 32 * KIB
FLOPS = 2 * S * (K * N + K * H + H * N)


def tile_picked_dmpnn8_relu_p_kernel(
    tc, x_words, x_scales, w1, w2, w3, offs, in1, in2, rev, out
):
    nc = tc.nc
    with ExitStack() as ctx:
        keep = ctx.enter_context(tc.tile_pool(name="keep", bufs=1))
        psum = ctx.enter_context(tc.psum_pool(name="psum", bufs=1))

        shared = ctx.enter_context(tc.tile_pool(name="shared", bufs=1))

        def sbuf(name, shape, dtype, tag=None):
            return keep.tile([P] + shape, dtype, name=name, tag=tag or name, align_bytes=256)

        def placed(name, shape, dtype, offset):
            return shared.tile([P] + shape, dtype, name=name, align_bytes=256, offset=offset)

        offs_sb = sbuf("offs_sb", [S // PER_COL], U16)
        in1_sb = sbuf("in1_sb", [S // PER_COL], U16)
        in2_sb = sbuf("in2_sb", [S // PER_COL], U16)
        rev_sb = sbuf("rev_sb", [S // PER_COL], U16)
        words_all = placed("words_all", [T], I32, 1 * KIB)
        scales_all = placed("scales_all", [T], U8, 13 * KIB)
        w1_raw = sbuf("w1_raw", [PACK, H], F32)
        y = [placed("y%d" % t, [S], F32, (t + 1) * APART) for t in range(PACK)]

        nc.vector.memset(scales_all[:].bitcast(I32), 0)
        w1_rows = w1.rearrange("(p j) c -> p j c", j=PACK)
        x_rows = x_words[0].rearrange("p n t -> p (n t)").bitcast(I32)
        nc.sync.dma_start(out=words_all[:, 0 : T // 2], in_=x_rows[:, 0 : T // 2])
        nc.sync.dma_start(offs_sb[:], offs)
        nc.sync.dma_start(out=scales_all[0:P:8, :].bitcast(I32), in_=x_scales[0].bitcast(I32))
        nc.sync.dma_start(out=words_all[:, T // 2 : T], in_=x_rows[:, T // 2 : T])
        nc.sync.dma_start(rev_sb[:], rev)
        nc.sync.dma_start(out=w1_raw[:], in_=w1_rows)
        nc.sync.dma_start(in2_sb[:], in2)
        nc.sync.dma_start(in1_sb[:], in1)

        x_sc = sbuf("x_sc", [S], U8)
        nc.vector.memset(x_sc[:].bitcast(I32), 0)
        x_q = sbuf("x_q", [S], U32)
        picked_sc = sbuf("picked_sc", [S], U8)
        nc.vector.tensor_copy(picked_sc[:], scales_all[:].indirect(offs_sb[:]))
        for r in range(4):
            nc.sync.dma_start(out=x_sc[r:P:32, :].bitcast(I32), in_=picked_sc[8 * r : P : 32, :].bitcast(I32))
        nc.vector.tensor_copy(x_q[:], words_all[:].bitcast(U32).indirect(offs_sb[:]))
        x_mx = (x_q, x_sc)
        w2_raw = placed("w2_raw", [PACK, N], F32, 13 * KIB)
        w3_raw = placed("w3_raw", [PACK, N], F32, 1 * KIB)
        nc.sync.dma_start(out=w2_raw[:], in_=w2.rearrange("(p j) c -> p j c", j=PACK))
        w3_rows = w3.rearrange("(g t i) c -> i g t c", t=PACK, i=4)
        for i in range(4):
            nc.sync.dma_start(out=w3_raw[i:P:4], in_=w3_rows[i])

        def quantize(name, grouped, width, tag=None):
            codes = sbuf(name + "_codes", [width], U32, tag)
            scales = sbuf(name + "_scales", [width], U8)
            nc.vector.quantize_mx(out=codes[:].bitcast(FP8X4), scales=scales[:], in_=grouped)
            return codes, scales

        def mx(dst, left, m, right, cols, start, stop):
            nc.tensor.matmul_mx(
                out=dst,
                lhsT=left[0][:, m * P : (m + 1) * P].bitcast(FP8X4),
                lhsT_scale=left[1][:, m * P : (m + 1) * P],
                rhs=right[0][:, cols].bitcast(FP8X4),
                rhs_scale=right[1][:, cols],
                start=start,
                stop=stop,
            )

        w1_grp = [sbuf("w1_grp%d" % t, [P, PACK], BF16) for t in range(PACK)]
        w1_cols = w1_raw[:].rearrange("p j (g t i) -> p t g j i", t=PACK, i=4)

        def cast_w1(copy, t):
            copy(w1_grp[t][:].rearrange("p (g i) j -> p g j i", i=4), w1_cols[:, t])

        def quantize_w1(t, tag=None):
            return quantize("w1_%d" % t, w1_grp[t][:].rearrange("p m j -> p (m j)"), P, tag)

        def y_piece(i, t, c0, n, codes, copy):
            bank = psum.tile([P, n], F32, name="y%d_%d" % (t, c0), tag="bank%d" % i)
            mx(bank[:], codes, 0, x_mx, slice(c0, c0 + n), True, True)
            copy(y[t][:, c0 : c0 + n], bank[:])

        cast_w1(nc.scalar.copy, 3)
        cast_w1(nc.vector.tensor_copy, 0)
        cast_w1(nc.vector.tensor_copy, 1)
        w1_mx = {0: quantize_w1(0)}
        cast_w1(nc.vector.tensor_copy, 2)
        w1_mx.update({t: quantize_w1(t) for t in (1, 3)})
        for q in range(4):
            y_piece(q, 0, q * QUARTER, QUARTER, w1_mx[0], (nc.vector.tensor_copy, nc.scalar.copy)[q // 2])
        w1_mx.update({2: quantize_w1(2, "w1_0_codes")})

        def entries(tile, c0, n):
            return tile[:, c0 // PER_COL : (c0 + n) // PER_COL]

        spans = ((0, HALF), (HALF, QUARTER), (HALF + QUARTER, QUARTER))
        part = {}

        back = {}

        def fetch_rev(h, t):
            back[h, t] = placed("back%d_%d" % (h, t), [HALF], F32, 5 * APART + (h * PACK + t) * KIB)
            nc.scalar.activation(back[h, t][:], y[t][:].indirect(entries(rev_sb, h * HALF, HALF)), COPY)

        def fetch_in2(h, t):
            nc.scalar.activation(other[h][:, t, :], y[t][:].indirect(entries(in2_sb, h * HALF, HALF)), COPY)

        def fetch_in1(c0, n, t):
            h, at = divmod(c0, HALF)
            nc.vector.tensor_tensor(part[h][:, t, at : at + n], y[t][:].indirect(entries(in1_sb, c0, n)), back[h, t][:, at : at + n], SUB)

        def weight(name, raw, between):
            grp = [sbuf("%s_grp%d" % (name, h), [HALF, PACK], BF16) for h in range(2)]
            for h in range(2):
                nc.vector.tensor_copy(
                    grp[h][:].rearrange("p (c i) j -> p c j i", i=4),
                    raw[:, :, h * HALF : (h + 1) * HALF].rearrange("p j (c i) -> p c j i", i=4),
                )
            codes = sbuf(name + "_codes", [N], U32)
            scales = sbuf(name + "_scales", [N], U8)
            for h in range(2):
                if h:
                    between()
                cols = slice(h * HALF, (h + 1) * HALF)
                nc.vector.quantize_mx(out=codes[:, cols].bitcast(FP8X4), scales=scales[:, cols], in_=grp[h][:].rearrange("p c j -> p (c j)"))
            return codes, scales

        def sum_z(i, offset=None):
            c0, n = spans[i]
            h, at = divmod(c0, HALF)
            name = "z%d_grp" % i
            grp = sbuf(name, [n, PACK], BF16) if offset is None else placed(name, [n, PACK], BF16, offset)
            nc.vector.tensor_tensor(
                grp[:].rearrange("p (c i) t -> p c t i", i=4),
                part[h][:, :, at : at + n].rearrange("p t (c i) -> p c t i", i=4),
                other[h][:, :, at : at + n].rearrange("p t (c i) -> p c t i", i=4),
                ADD,
            )
            return grp[:].rearrange("p c t -> p (c t)")

        out_rows = out.rearrange("(u p) j -> p u j", p=P)

        def relu_scalar(dst, src):
            nc.scalar.activation(dst, src, RELU)

        def relu_vector(dst, src):
            nc.vector.tensor_scalar_max(dst, src, 0.0)

        def take_banks(i, first):
            return [psum.tile([P, spans[i][1]], F32, name="o%d_bank%d" % (i, u), tag="bank%d" % (first + u)) for u in range(PACK)]

        def h0_pass(i, bank, u, opens):
            c0, n = spans[i]
            mx(bank[:], w2_mx, u, x_mx, slice(c0, c0 + n), opens, not opens)

        def open_banks(i, first, count):
            banks = take_banks(i, first)
            for u in range(count):
                h0_pass(i, banks[u], u, True)
            return banks

        def finish(i, banks, opened, z_mx, relus, stores):
            c0, n = spans[i]
            res = sbuf("res%d" % i, [PACK, n], F32)
            for u in range(PACK):
                mx(banks[u][:], w3_mx, u, z_mx, slice(0, n), u >= opened, u < opened)
                if u >= opened:
                    h0_pass(i, banks[u], u, False)
                relus[u](res[:, u, :], banks[u][:])
                if u in stores:
                    rows_out = slice(stores[u], u + 1)
                    nc.sync.dma_start(out=out_rows[:, rows_out, c0 : c0 + n], in_=res[:, rows_out, :])

        other = {}
        y_piece(4, 1, 0, HALF, w1_mx[1], nc.vector.tensor_copy)
        y_piece(7, 1, HALF, HALF, w1_mx[1], nc.vector.tensor_copy)
        fetch_rev(0, 0)
        y_piece(5, 2, 0, S, w1_mx[2], nc.scalar.copy)
        y_piece(6, 3, 0, S, w1_mx[3], nc.scalar.copy)

        def first_in1():
            part[0] = placed("part0", [PACK, HALF], F32, 17 * KIB)
            fetch_in1(0, HALF, 0)

        w2_mx = weight("w2", w2_raw, first_in1)
        other[0] = sbuf("other0", [PACK, HALF], F32)
        for t in (1, 2, 3):
            fetch_rev(0, t)
        for t in range(PACK):
            fetch_in2(0, t)
        for t in (1, 2, 3):
            fetch_in1(0, HALF, t)
        w3_mx = weight("w3", w3_raw, lambda: None)
        for t in range(PACK):
            fetch_rev(1, t)
        banks1 = open_banks(1, 4, PACK)
        other[1] = placed("other1", [PACK, HALF], F32, 6 * KIB)
        part[1] = placed("part1", [PACK, HALF], F32, 2 * KIB)
        for t in (0, 1, 2):
            fetch_in2(1, t)
        nc.scalar.activation(other[1][:, 3, QUARTER:HALF], y[3][:].indirect(entries(in2_sb, *spans[2])), COPY)
        nc.vector.tensor_copy(other[1][:, 3, 0:QUARTER], y[3][:].indirect(entries(in2_sb, *spans[1])))
        z0_grp = sum_z(0, 0)
        fetch_in1(HALF, HALF, 0)
        z0_mx = quantize("z0", z0_grp, spans[0][1])
        finish(0, take_banks(0, 0), 0, z0_mx, (relu_scalar,) * 4, {1: 0, 3: 2})
        banks2 = open_banks(2, 0, PACK - 1)
        fetch_in1(HALF, HALF, 1)
        fetch_in1(*spans[1], 2)
        fetch_in1(*spans[1], 3)
        fetch_in1(*spans[2], 2)
        z1_grp = sum_z(1)
        fetch_in1(*spans[2], 3)
        z1_mx = quantize("z1", z1_grp, spans[1][1])
        z2_grp = sum_z(2)
        finish(1, banks1, PACK, z1_mx, (relu_vector, relu_scalar) * 2, {1: 0, 3: 2})
        z2_mx = quantize("z2", z2_grp, spans[2][1])
        finish(2, banks2, PACK - 1, z2_mx, (relu_scalar, relu_vector) * 2, {0: 0, 1: 1, 3: 2})
